import numpy as np
import ml_dtypes


def mxq(x, axis, fmt="e4m3"):
    dtype, down = {"e4m3": (ml_dtypes.float8_e4m3fn, 7), "e5m2": (ml_dtypes.float8_e5m2, 14)}[fmt]
    v = np.moveaxis(np.asarray(x, np.float32).astype(ml_dtypes.bfloat16).astype(np.float64), axis, -1)
    blocks = v.reshape(v.shape[:-1] + (-1, 32))
    amax = np.abs(blocks).max(-1, keepdims=True)
    byte = np.maximum(np.where(amax > 0, np.frexp(amax)[1] - 1 + 127, 0) - down, 1)
    scale = np.exp2(byte - 127.0)
    codes = (blocks / scale).astype(np.float32).astype(dtype).astype(np.float64)
    return np.moveaxis((codes * scale).reshape(v.shape), -1, axis)


WIDE = False


def mx_kscale(k):
    if not WIDE:
        return np.ones(k)
    levels = np.array([10, -10, 5, -5, 0])
    if k % 512:
        return np.exp2(np.random.permutation(np.resize(levels, k // 32))).repeat(32)
    a = np.empty((k // 512, 16))
    for p in range(k // 512):
        a[p, :8] = np.random.permutation(np.resize(levels, 8))
        for g in range(8):
            far = levels[np.abs(levels - a[p, g]) >= 10]
            a[p, g + 8] = far[np.random.randint(len(far))]
    return np.exp2(a.ravel()).repeat(32)


def f64(x):
    return np.asarray(x).astype(np.float64)


def striped(idx):
    return np.tile(idx.reshape(-1, 16).T, (8, 1)).astype(np.uint16)


def unstriped(offs):
    return offs[:16].T.reshape(-1).astype(np.int64)


E2M1 = np.array([0.0, 0.5, 1.0, 1.5, 2.0, 3.0, 4.0, 6.0, -0.0, -0.5, -1.0, -1.5, -2.0, -3.0, -4.0, -6.0])


def pack_weight(w, fmt):
    k, n = w.shape
    w = f64(np.asarray(w, np.float32).astype(ml_dtypes.bfloat16)).reshape(k // 32, 32, n)
    amax = np.abs(w).max(1)
    if fmt == "e4m3":
        byte = np.frexp(amax)[1] - 1 + 127 - 7
    else:
        mant, ex = np.frexp(amax / 6.0)
        byte = np.where(mant > 0.5, ex, ex - 1) + 127
    byte = np.clip(np.where(amax > 0, byte, 1), 1, 254)
    scaled = (w * np.exp2(127.0 - byte)[:, None, :]).reshape(k, n).astype(np.float32)
    by_word = np.ascontiguousarray(scaled.reshape(k // 512, 128, 4, n).transpose(0, 1, 3, 2))
    if fmt == "e4m3":
        words = by_word.astype(ml_dtypes.float8_e4m3fn).view(np.uint8)
    else:
        c = by_word.astype(ml_dtypes.float4_e2m1fn).view(np.uint8) & 0xF
        words = (c[..., 0::2] | (c[..., 1::2] << 4)).reshape(k // 512, 128, 2 * n)
    return np.ascontiguousarray(words), np.ascontiguousarray(byte.astype(np.uint8).reshape(k // 512, 16, n))


def unpack_weight(words, scales, fmt):
    g, _, n = scales.shape
    words = np.ascontiguousarray(words).reshape(g, 128, n, -1)
    if fmt == "e4m3":
        vals = words.view(ml_dtypes.float8_e4m3fn).astype(np.float64)
    else:
        nib = np.empty((g, 128, n, 4), np.uint8)
        nib[..., 0::2] = words & 0xF
        nib[..., 1::2] = words >> 4
        vals = E2M1[nib]
    vals = vals * np.repeat(np.exp2(scales.astype(np.float64) - 127.0), 8, axis=1)[..., None]
    return vals.transpose(0, 1, 3, 2).reshape(g * 512, n)


def silu(v):
    return v / (1.0 + np.exp(-np.maximum(v, -700.0)))


K, T, E, C, H, N = 1024, 2048, 4, 256, 512, 128
R = 2


def by_expert(wq, xq):
    return np.concatenate([wq[e].T @ xq[:, e * C:(e + 1) * C] for e in range(E)], axis=1)


def setup_inputs():
    n = np.random.standard_normal
    s = mx_kscale(K)[:, None]
    u = mx_kscale(H)
    slot_token = np.concatenate([r * (T // R) + np.random.permutation(T // R)[:C // R] for e in range(E) for r in range(R)])
    w1 = [pack_weight(m, "e2m1") for m in n((E, K, H)) / np.sqrt(K) / s[None]]
    w3 = [pack_weight(m, "e2m1") for m in n((E, K, H)) / np.sqrt(K) / s[None] * u[None, None, :]]
    w2 = [pack_weight(m, "e2m1") for m in n((E, H, N)) / np.sqrt(H) / u[None, :, None]]
    x = pack_weight(n((K, T)) * s, "e4m3")
    return {
        "x_words": x[0],
        "x_scales": x[1],
        "w1_words": np.stack([m[0] for m in w1]),
        "w1_scales": np.stack([m[1] for m in w1]),
        "w3_words": np.stack([m[0] for m in w3]),
        "w3_scales": np.stack([m[1] for m in w3]),
        "w2_words": np.stack([m[0] for m in w2]),
        "w2_scales": np.stack([m[1] for m in w2]),
        "offs": striped(slot_token),
    }


def reference(x_words, x_scales, w1_words, w1_scales, w3_words, w3_scales, w2_words, w2_scales, offs):
    idx = unstriped(offs)
    w1 = np.stack([unpack_weight(w1_words[e], w1_scales[e], "e2m1") for e in range(E)])
    w3 = np.stack([unpack_weight(w3_words[e], w3_scales[e], "e2m1") for e in range(E)])
    w2 = np.stack([unpack_weight(w2_words[e], w2_scales[e], "e2m1") for e in range(E)])
    xq = unpack_weight(x_words, x_scales, "e4m3")[:, idx]
    h = silu(by_expert(w1, xq))
    h = h * by_expert(w3, xq)
    y = by_expert(w2, mxq(h, 0, "e4m3"))
    return y.reshape(N, E, R, C // R).transpose(0, 2, 1, 3).reshape(N, E * C)

@@ -1,0 +1,234 @@
+from contextlib import ExitStack
+
+import concourse.mybir as mybir
+from concourse.masks import make_identity
+
+K, T, E, C, H, N = 1024, 2048, 4, 256, 512, 128
+RANKS = 2
+SLOTS = E * C
+P = 128
+PASSES = K // 512
+TILES = SLOTS // P
+EARLY = 4
+FLOPS = 2 * SLOTS * (2 * K * H + H * N)
+
+F32 = mybir.dt.float32
+BF16 = mybir.dt.bfloat16
+I32 = mybir.dt.int32
+U32 = mybir.dt.uint32
+U16 = mybir.dt.uint16
+U8 = mybir.dt.uint8
+FP8X4 = mybir.dt.float8_e4m3fn_x4
+FP4X4 = mybir.dt.float4_e2m1fn_x4
+SILU = mybir.ActivationFunctionType.Silu
+MULT = mybir.AluOpType.mult
+
+
+def tile_moe_pke_glu_silu_kernel(
+    tc, x_words, x_scales, w1_words, w1_scales, w3_words, w3_scales, w2_words, w2_scales, offs, out
+):
+    nc = tc.nc
+    with ExitStack() as ctx:
+        keep = ctx.enter_context(tc.tile_pool(name="keep", bufs=1))
+        work = ctx.enter_context(tc.tile_pool(name="work", bufs=2))
+        psum = ctx.enter_context(tc.psum_pool(name="psum", bufs=8))
+
+        offsets = keep.tile([P, SLOTS // 16], U16, name="offsets")
+        nc.sync.dma_start(offsets[:], offs)
+
+        xs_window = keep.tile([P, T], U8, name="xs_window", align_bytes=64)
+        xs_slots = keep.tile([P, SLOTS], U8, name="xs_slots", align_bytes=64)
+        xs_pass1 = keep.tile([P, SLOTS], U8, name="xs_pass1", align_bytes=64)
+        ident = keep.tile([P, P], F32, name="ident")
+
+        nc.vector.memset(xs_window[:].bitcast(I32), 0)
+        xs_rows = x_scales.bitcast(I32)
+        for q in range(4):
+            nc.sync.dma_start(xs_window[32 * q : 32 * q + 8, :].bitcast(I32), xs_rows[:, 4 * q : 4 * q + 4, :])
+
+        make_identity(nc, ident[:])
+        w1_plane = keep.tile([P, E * PASSES * H], U8, name="w1_plane", align_bytes=64)
+        w3_plane = keep.tile([P, E * PASSES * H], U8, name="w3_plane", align_bytes=64)
+
+        def clear_then_open(plane, name):
+            with tc.tile_pool(name=name + "_zero", bufs=1) as scratch:
+                zero = scratch.tile([P, 1], I32, name="zero")
+                nc.vector.memset(zero[:], 0)
+                nc.vector.tensor_copy(plane[:].bitcast(I32), zero[:].to_broadcast([P, E * PASSES * H // 4]))
+            return ctx.enter_context(tc.tile_pool(name=name, bufs=1))
+
+        def load_plane(queue, plane, scales):
+            rows = scales.bitcast(I32).rearrange("e s (q r) i -> r q (e s) i", r=4)
+            for r in range(4):
+                queue.dma_start(plane[r:P:32, :].bitcast(I32).rearrange("q (g i) -> q g i", g=rows.shape[2]), rows[r])
+
+        loads = clear_then_open(w1_plane, "loads")
+        x0_tile = loads.tile([P, T], I32, name="x0", align_bytes=64)
+        w1a_tile = loads.tile([P, 4 * H], U8, name="w1a", align_bytes=64)
+        late = clear_then_open(w3_plane, "late")
+        w2_plane = late.tile([P, E * N], U8, name="w2_plane", align_bytes=64)
+        nc.vector.memset(w2_plane[:].bitcast(I32), 0)
+        nc.vector.memset(xs_pass1[:].bitcast(I32), 0)
+        warm_in = keep.tile([P, 1], F32, name="warm_in")
+        warm_out = keep.tile([P, 1], F32, name="warm_out")
+        nc.vector.memset(warm_in[:], 0.0)
+        nc.scalar.activation(warm_out[:], warm_in[:], SILU)
+
+        def load_tokens(s):
+            words = x0_tile if s == 0 else late.tile([P, T], I32, name="x%d" % s, align_bytes=64)
+            nc.sync.dma_start(words[:], x_words[s].rearrange("p t r -> p (t r)").bitcast(I32))
+            return words
+
+        weights = {}
+
+        def load_weights(which, source, pieces):
+            e0, e1, s0, s1 = pieces
+            count = (e1 - e0) * (s1 - s0)
+            tile = w1a_tile if (which, e0, s0) == (1, 0, 0) else late.tile([P, count * 2 * H], U8, name="w%d_%d_%d" % (which, e0, s0), align_bytes=64)
+            words = source.bitcast(I32)
+            if count == 1:
+                nc.sync.dma_start(tile[:].bitcast(I32), words[e0, s0])
+            elif e1 - e0 == 1:
+                nc.sync.dma_start(tile[:].bitcast(I32).rearrange("p (g b) -> p g b", g=count), words[e0].rearrange("s p b -> p s b"))
+            else:
+                nc.sync.dma_start(tile[:].bitcast(I32).rearrange("p (g b) -> p g b", g=count), words[e0:e1, s0].rearrange("e p b -> p e b"))
+            for j in range(count):
+                weights[(which, e0 + j // (s1 - s0), s0 + j % (s1 - s0))] = tile[:, j * 2 * H : (j + 1) * 2 * H]
+
+        x_window = [load_tokens(0)]
+        load_weights(1, w1_words, (0, 2, 0, 1))
+        load_plane(nc.sync, w1_plane, w1_scales)
+        x_window.append(load_tokens(1))
+        load_weights(1, w1_words, (0, 2, 1, 2))
+        load_weights(3, w3_words, (0, 1, 0, 2))
+        load_plane(nc.sync, w3_plane, w3_scales)
+        load_weights(3, w3_words, (1, 2, 0, 2))
+        load_weights(1, w1_words, (2, 3, 0, 2))
+        load_weights(3, w3_words, (2, 3, 0, 2))
+        w2_tile = late.tile([P, E * 2 * N], U8, name="w2_tile", align_bytes=64)
+        nc.sync.dma_start(w2_tile[:].bitcast(I32).rearrange("p (e b) -> p e b", e=E), w2_words.bitcast(I32).rearrange("e s p b -> p (e s) b"))
+        load_plane(nc.sync, w2_plane, w2_scales)
+        load_weights(1, w1_words, (3, 4, 0, 2))
+        load_weights(3, w3_words, (3, 4, 0, 2))
+
+        nc.vector.tensor_copy(xs_slots[:], xs_window[:].indirect(offsets[:]))
+        nc.gpsimd.dma_start(xs_pass1[0:100, :].bitcast(I32), xs_slots[4:104, :].bitcast(I32))
+        x_plane = [xs_slots, xs_pass1]
+
+        gathered = {}
+
+        def gather_words(s, e):
+            tile = keep.tile([P, C], U32, name="xg%d_%d" % (s, e), align_bytes=64)
+            nc.vector.tensor_copy(tile[:], x_window[s][:].bitcast(U32).indirect(offsets[:, e * C // 16 : (e + 1) * C // 16]))
+            gathered[(s, e)] = tile
+
+        planes = {1: w1_plane, 3: w3_plane}
+        sums = {}
+
+        def first_layer(t, which, s):
+            e, half = divmod(t, 2)
+            if s == 0:
+                sums[(t, which)] = psum.tile([P, H], F32, name="bank")
+            g = e * PASSES + s
+            nc.tensor.matmul_mx(
+                out=sums[(t, which)][:],
+                lhsT=gathered[(s, e)][:, half * P : (half + 1) * P].bitcast(FP8X4),
+                lhsT_scale=x_plane[s][:, t * P : (t + 1) * P],
+                rhs=weights[(which, e, s)].bitcast(FP4X4),
+                rhs_scale=planes[which][:, g * H : (g + 1) * H],
+                start=(s == 0),
+                stop=(s == PASSES - 1),
+            )
+
+        hidden = {}
+
+        order = "c (p u d) -> c u p d"
+        gates = {}
+
+        def silu(t):
+            gates[t] = work.tile([P, 2, P, 2], F32, name="gate", bufs=4)
+            nc.scalar.activation(gates[t][:], sums[(t, 1)][:].rearrange(order, u=2, d=2), SILU)
+
+        def multiply(t):
+            hidden[t] = work.tile([P, 2, P, 2], BF16, name="hidden", bufs=4)
+            nc.vector.tensor_tensor(hidden[t][:], gates[t][:], sums[(t, 3)][:].rearrange(order, u=2, d=2), MULT)
+
+        packed = {}
+
+        def turn(tiles):
+            width = len(tiles) * P
+            bank = psum.tile([P, H], F32, name="bank")
+            for j, t in enumerate(tiles):
+                pairs = hidden[t][:].rearrange("c u p d -> c (u p d)").bitcast(F32)
+                for u in range(2):
+                    at = u * width + j * P
+                    nc.tensor.transpose(bank[:, at : at + P], pairs[:, u * P : (u + 1) * P], ident[:])
+            rows = work.tile([P, 4 * C], BF16, name="rows", align_bytes=64)
+            nc.scalar.copy(
+                rows[:, : 4 * width].bitcast(F32).rearrange("p (c u) -> p c u", u=2),
+                bank[:, : 2 * width].rearrange("p (u c) -> p c u", u=2),
+            )
+            codes = work.tile([P, C], U32, name="codes", align_bytes=64)
+            scales = work.tile([P, C], U8, name="scales", align_bytes=64)
+            nc.vector.quantize_mx(out=codes[:, :width].bitcast(FP8X4), scales=scales[:, :width], in_=rows[:, : 4 * width])
+            packed[tiles] = (codes, scales)
+
+        by_rank = out.rearrange("n (m e u) -> n e m u", m=RANKS, e=E)
+
+        def second_layer(tiles):
+            width = len(tiles) * P
+            e = tiles[0] // 2
+            codes, scales = packed[tiles]
+            bank = psum.tile([P, H], F32, name="bank")
+            nc.tensor.matmul_mx(
+                out=bank[:, :width],
+                lhsT=w2_tile[:, e * 2 * N : (e + 1) * 2 * N].bitcast(FP4X4),
+                lhsT_scale=w2_plane[:, e * N : (e + 1) * N],
+                rhs=codes[:, :width].bitcast(FP8X4),
+                rhs_scale=scales[:, :width],
+                start=True,
+                stop=True,
+            )
+            result = work.tile([P, C], F32, name="result", bufs=3)
+            nc.scalar.copy(result[:, :width], bank[:, :width])
+            m = tiles[0] % 2
+            if len(tiles) == 1:
+                nc.sync.dma_start(by_rank[:, e, m, :], result[:, :P])
+            else:
+                nc.sync.dma_start(by_rank[:, e], result[:].rearrange("n (m u) -> n m u", u=P))
+
+        for e in range(E):
+            gather_words(0, e)
+        for t in range(EARLY):
+            first_layer(t, 1, 0)
+        for e in range(E):
+            gather_words(1, e)
+        for t in range(EARLY):
+            first_layer(t, 1, 1)
+            silu(t)
+        for t in range(EARLY):
+            first_layer(t, 3, 0)
+            first_layer(t, 3, 1)
+            multiply(t)
+
+        def whole_tile(t):
+            for s in range(PASSES):
+                first_layer(t, 1, s)
+            silu(t)
+            for s in range(PASSES):
+                first_layer(t, 3, s)
+            multiply(t)
+
+        turn((0, 1))
+        whole_tile(4)
+        second_layer((0, 1))
+        turn((2, 3))
+        whole_tile(5)
+        second_layer((2, 3))
+        whole_tile(6)
+        turn((4, 5))
+        whole_tile(7)
+        second_layer((4, 5))
+        for t in (6, 7):
+            turn((t,))
+            second_layer((t,))

@@ -9,7 +9,6 @@ SLOTS = E * C
 P = 128
 PASSES = K // 512
 TILES = SLOTS // P
-EARLY = 4
 FLOPS = 2 * SLOTS * (2 * K * H + H * N)
 
 F32 = mybir.dt.float32
@@ -22,6 +21,7 @@ FP8X4 = mybir.dt.float8_e4m3fn_x4
 FP4X4 = mybir.dt.float4_e2m1fn_x4
 SILU = mybir.ActivationFunctionType.Silu
 MULT = mybir.AluOpType.mult
+ROW = 2 * H
 
 
 def tile_moe_pke_glu_silu_kernel(
@@ -39,88 +39,92 @@ def tile_moe_pke_glu_silu_kernel(
         xs_window = keep.tile([P, T], U8, name="xs_window", align_bytes=64)
         xs_slots = keep.tile([P, SLOTS], U8, name="xs_slots", align_bytes=64)
         xs_pass1 = keep.tile([P, SLOTS], U8, name="xs_pass1", align_bytes=64)
-        ident = keep.tile([P, P], F32, name="ident")
-
-        nc.vector.memset(xs_window[:].bitcast(I32), 0)
-        xs_rows = x_scales.bitcast(I32)
-        for q in range(4):
-            nc.sync.dma_start(xs_window[32 * q : 32 * q + 8, :].bitcast(I32), xs_rows[:, 4 * q : 4 * q + 4, :])
-
-        make_identity(nc, ident[:])
         w1_plane = keep.tile([P, E * PASSES * H], U8, name="w1_plane", align_bytes=64)
         w3_plane = keep.tile([P, E * PASSES * H], U8, name="w3_plane", align_bytes=64)
+        ident = keep.tile([P, P], F32, name="ident")
 
-        def clear_then_open(plane, name):
-            with tc.tile_pool(name=name + "_zero", bufs=1) as scratch:
-                zero = scratch.tile([P, 1], I32, name="zero")
-                nc.vector.memset(zero[:], 0)
-                nc.vector.tensor_copy(plane[:].bitcast(I32), zero[:].to_broadcast([P, E * PASSES * H // 4]))
-            return ctx.enter_context(tc.tile_pool(name=name, bufs=1))
+        make_identity(nc, ident[:])
 
-        def load_plane(queue, plane, scales):
+        def clear(plane, zero):
+            words = plane[:].bitcast(I32)
+            nc.vector.tensor_copy(words, zero[:].to_broadcast(words.shape))
+
+        def load_plane(plane, scales):
             rows = scales.bitcast(I32).rearrange("e s (q r) i -> r q (e s) i", r=4)
             for r in range(4):
-                queue.dma_start(plane[r:P:32, :].bitcast(I32).rearrange("q (g i) -> q g i", g=rows.shape[2]), rows[r])
+                nc.sync.dma_start(plane[r:P:32, :].bitcast(I32).rearrange("q (g i) -> q g i", g=rows.shape[2]), rows[r])
 
-        loads = clear_then_open(w1_plane, "loads")
-        x0_tile = loads.tile([P, T], I32, name="x0", align_bytes=64)
-        w1a_tile = loads.tile([P, 4 * H], U8, name="w1a", align_bytes=64)
-        late = clear_then_open(w3_plane, "late")
-        w2_plane = late.tile([P, E * N], U8, name="w2_plane", align_bytes=64)
-        nc.vector.memset(w2_plane[:].bitcast(I32), 0)
-        nc.vector.memset(xs_pass1[:].bitcast(I32), 0)
+        def load_rows(tile, rows):
+            nc.sync.dma_start(tile.bitcast(I32).rearrange("p (g b) -> p g b", g=rows.shape[0]), rows.rearrange("g p b -> p g b"))
+
+        x_rows = x_words.rearrange("s p t r -> s p (t r)").bitcast(I32)
+        w1_rows = w1_words.bitcast(I32)
+        w3_rows = w3_words.bitcast(I32)
+
+        with tc.tile_pool(name="first_zero", bufs=1) as scratch:
+            zero = scratch.tile([P, 1], I32, name="zero")
+            nc.vector.memset(zero[:], 0)
+            nc.vector.memset(xs_window[:].bitcast(I32), 0)
+            xs_rows = x_scales.bitcast(I32)
+            for q in range(4):
+                nc.sync.dma_start(xs_window[32 * q : 32 * q + 8, :].bitcast(I32), xs_rows[:, 4 * q : 4 * q + 4, :])
+            clear(xs_pass1, zero)
+        first = ctx.enter_context(tc.tile_pool(name="first", bufs=1))
+        x0 = first.tile([P, T + E * 3 * N // 4], I32, name="x0", align_bytes=64, offset=0)[:, :T]
+        w1_pass0 = first.tile([P, E * ROW], U8, name="w1_pass0", align_bytes=64, offset=4 * T + E * 3 * N)
+        nc.sync.dma_start(x0, x_rows[0])
+        load_rows(w1_pass0[:], w1_rows[:, 0])
+        with tc.tile_pool(name="second_zero", bufs=1) as scratch:
+            zero = scratch.tile([P, 1], I32, name="zero")
+            nc.vector.memset(zero[:], 0)
+            nc.vector.memset(w1_plane[:].bitcast(I32), 0)
+            load_plane(w1_plane, w1_scales)
+            clear(w3_plane, zero)
+        second = ctx.enter_context(tc.tile_pool(name="second", bufs=1))
+        x1 = second.tile([P, T], I32, name="x1", align_bytes=64)
+        nc.sync.dma_start(x1[:], x_rows[1])
+        w1_pass1 = []
+        for pair in range(2):
+            w1_pass1.append(second.tile([P, 2 * ROW], U8, name="w1_pass1_%d" % pair, align_bytes=64))
+            load_rows(w1_pass1[pair][:], w1_rows[2 * pair : 2 * pair + 2, 1])
+        load_plane(w3_plane, w3_scales)
+
         warm_in = keep.tile([P, 1], F32, name="warm_in")
         warm_out = keep.tile([P, 1], F32, name="warm_out")
         nc.vector.memset(warm_in[:], 0.0)
         nc.scalar.activation(warm_out[:], warm_in[:], SILU)
 
-        def load_tokens(s):
-            words = x0_tile if s == 0 else late.tile([P, T], I32, name="x%d" % s, align_bytes=64)
-            nc.sync.dma_start(words[:], x_words[s].rearrange("p t r -> p (t r)").bitcast(I32))
-            return words
-
-        weights = {}
-
-        def load_weights(which, source, pieces):
-            e0, e1, s0, s1 = pieces
-            count = (e1 - e0) * (s1 - s0)
-            tile = w1a_tile if (which, e0, s0) == (1, 0, 0) else late.tile([P, count * 2 * H], U8, name="w%d_%d_%d" % (which, e0, s0), align_bytes=64)
-            words = source.bitcast(I32)
-            if count == 1:
-                nc.sync.dma_start(tile[:].bitcast(I32), words[e0, s0])
-            elif e1 - e0 == 1:
-                nc.sync.dma_start(tile[:].bitcast(I32).rearrange("p (g b) -> p g b", g=count), words[e0].rearrange("s p b -> p s b"))
-            else:
-                nc.sync.dma_start(tile[:].bitcast(I32).rearrange("p (g b) -> p g b", g=count), words[e0:e1, s0].rearrange("e p b -> p e b"))
-            for j in range(count):
-                weights[(which, e0 + j // (s1 - s0), s0 + j % (s1 - s0))] = tile[:, j * 2 * H : (j + 1) * 2 * H]
-
-        x_window = [load_tokens(0)]
-        load_weights(1, w1_words, (0, 2, 0, 1))
-        load_plane(nc.sync, w1_plane, w1_scales)
-        x_window.append(load_tokens(1))
-        load_weights(1, w1_words, (0, 2, 1, 2))
-        load_weights(3, w3_words, (0, 1, 0, 2))
-        load_plane(nc.sync, w3_plane, w3_scales)
-        load_weights(3, w3_words, (1, 2, 0, 2))
-        load_weights(1, w1_words, (2, 3, 0, 2))
-        load_weights(3, w3_words, (2, 3, 0, 2))
-        w2_tile = late.tile([P, E * 2 * N], U8, name="w2_tile", align_bytes=64)
-        nc.sync.dma_start(w2_tile[:].bitcast(I32).rearrange("p (e b) -> p e b", e=E), w2_words.bitcast(I32).rearrange("e s p b -> p (e s) b"))
-        load_plane(nc.sync, w2_plane, w2_scales)
-        load_weights(1, w1_words, (3, 4, 0, 2))
-        load_weights(3, w3_words, (3, 4, 0, 2))
-
         nc.vector.tensor_copy(xs_slots[:], xs_window[:].indirect(offsets[:]))
-        nc.gpsimd.dma_start(xs_pass1[0:100, :].bitcast(I32), xs_slots[4:104, :].bitcast(I32))
+        nc.scalar.dma_start(xs_pass1[0:100, :].bitcast(I32), xs_slots[4:104, :].bitcast(I32))
         x_plane = [xs_slots, xs_pass1]
 
         gathered = {}
 
-        def gather_words(s, e):
+        def gather_words(s, window, e):
             tile = keep.tile([P, C], U32, name="xg%d_%d" % (s, e), align_bytes=64)
-            nc.vector.tensor_copy(tile[:], x_window[s][:].bitcast(U32).indirect(offsets[:, e * C // 16 : (e + 1) * C // 16]))
+            nc.vector.tensor_copy(tile[:], window.bitcast(U32).indirect(offsets[:, e * C // 16 : (e + 1) * C // 16]))
             gathered[(s, e)] = tile
+
+        for e in range(E):
+            gather_words(0, x0, e)
+
+        w2_all = first.tile([P, E * 2 * N], U8, name="w2_all", align_bytes=64, offset=4 * T)
+        w2_plane = first.tile([P, E * N], U8, name="w2_plane", align_bytes=64, offset=4 * T + E * 2 * N)
+        nc.vector.memset(w2_plane[:].bitcast(I32), 0)
+        w3_expert = []
+        for e in range(E):
+            w3_expert.append(first.tile([P, PASSES * ROW], U8, name="w3_%d" % e, align_bytes=64, offset=e * PASSES * ROW))
+            load_rows(w3_expert[e][:], w3_rows[e])
+            if e == 2:
+                load_rows(w2_all[:], w2_words.bitcast(I32)[:, 0])
+                load_plane(w2_plane, w2_scales)
+
+        def weights(which, e, s):
+            if which == 3:
+                return w3_expert[e][:, s * ROW : (s + 1) * ROW]
+            if s == 0:
+                return w1_pass0[:, e * ROW : (e + 1) * ROW]
+            return w1_pass1[e // 2][:, e % 2 * ROW : (e % 2 + 1) * ROW]
 
         planes = {1: w1_plane, 3: w3_plane}
         sums = {}
@@ -134,22 +138,23 @@ def tile_moe_pke_glu_silu_kernel(
                 out=sums[(t, which)][:],
                 lhsT=gathered[(s, e)][:, half * P : (half + 1) * P].bitcast(FP8X4),
                 lhsT_scale=x_plane[s][:, t * P : (t + 1) * P],
-                rhs=weights[(which, e, s)].bitcast(FP4X4),
+                rhs=weights(which, e, s).bitcast(FP4X4),
                 rhs_scale=planes[which][:, g * H : (g + 1) * H],
                 start=(s == 0),
                 stop=(s == PASSES - 1),
             )
 
-        hidden = {}
-
         order = "c (p u d) -> c u p d"
         gates = {}
+        hidden = {}
 
         def silu(t):
-            gates[t] = work.tile([P, 2, P, 2], F32, name="gate", bufs=4)
+            gates[t] = work.tile([P, 2, P, 2], F32, name="gate", bufs=TILES)
             nc.scalar.activation(gates[t][:], sums[(t, 1)][:].rearrange(order, u=2, d=2), SILU)
 
-        def multiply(t):
+        def gated(t):
+            for s in range(PASSES):
+                first_layer(t, 3, s)
             hidden[t] = work.tile([P, 2, P, 2], BF16, name="hidden", bufs=4)
             nc.vector.tensor_tensor(hidden[t][:], gates[t][:], sums[(t, 3)][:].rearrange(order, u=2, d=2), MULT)
 
@@ -175,14 +180,14 @@ def tile_moe_pke_glu_silu_kernel(
 
         by_rank = out.rearrange("n (m e u) -> n e m u", m=RANKS, e=E)
 
-        def second_layer(tiles):
+        def second_layer(tiles, copy_out):
             width = len(tiles) * P
             e = tiles[0] // 2
             codes, scales = packed[tiles]
             bank = psum.tile([P, H], F32, name="bank")
             nc.tensor.matmul_mx(
                 out=bank[:, :width],
-                lhsT=w2_tile[:, e * 2 * N : (e + 1) * 2 * N].bitcast(FP4X4),
+                lhsT=w2_all[:, e * 2 * N : (e + 1) * 2 * N].bitcast(FP4X4),
                 lhsT_scale=w2_plane[:, e * N : (e + 1) * N],
                 rhs=codes[:, :width].bitcast(FP8X4),
                 rhs_scale=scales[:, :width],
@@ -190,45 +195,33 @@ def tile_moe_pke_glu_silu_kernel(
                 stop=True,
             )
             result = work.tile([P, C], F32, name="result", bufs=3)
-            nc.scalar.copy(result[:, :width], bank[:, :width])
-            m = tiles[0] % 2
+            copy_out(result[:, :width], bank[:, :width])
             if len(tiles) == 1:
-                nc.sync.dma_start(by_rank[:, e, m, :], result[:, :P])
+                nc.sync.dma_start(by_rank[:, e, tiles[0] % 2, :], result[:, :P])
             else:
                 nc.sync.dma_start(by_rank[:, e], result[:].rearrange("n (m u) -> n m u", u=P))
 
-        for e in range(E):
-            gather_words(0, e)
-        for t in range(EARLY):
+        for t in range(TILES):
             first_layer(t, 1, 0)
         for e in range(E):
-            gather_words(1, e)
-        for t in range(EARLY):
+            gather_words(1, x1[:], e)
+        for t in range(TILES):
             first_layer(t, 1, 1)
             silu(t)
-        for t in range(EARLY):
-            first_layer(t, 3, 0)
-            first_layer(t, 3, 1)
-            multiply(t)
 
-        def whole_tile(t):
-            for s in range(PASSES):
-                first_layer(t, 1, s)
-            silu(t)
-            for s in range(PASSES):
-                first_layer(t, 3, s)
-            multiply(t)
-
+        for t in range(4):
+            gated(t)
         turn((0, 1))
-        whole_tile(4)
-        second_layer((0, 1))
+        gated(4)
+        gated(5)
         turn((2, 3))
-        whole_tile(5)
-        second_layer((2, 3))
-        whole_tile(6)
+        second_layer((0, 1), nc.scalar.copy)
+        gated(6)
+        gated(7)
         turn((4, 5))
-        whole_tile(7)
-        second_layer((4, 5))
-        for t in (6, 7):
-            turn((t,))
-            second_layer((t,))
+        second_layer((2, 3), nc.scalar.copy)
+        turn((6,))
+        turn((7,))
+        second_layer((4, 5), nc.vector.tensor_copy)
+        second_layer((6,), nc.scalar.copy)
+        second_layer((7,), nc.vector.tensor_copy)

@@ -115,7 +115,7 @@ def tile_moe_pke_glu_silu_kernel(
         for e in range(E):
             w3_expert.append(first.tile([P, PASSES * ROW], U8, name="w3_%d" % e, align_bytes=64, offset=e * PASSES * ROW))
             load_rows(w3_expert[e][:], w3_rows[e])
-            if e == 2:
+            if e == 3:
                 load_rows(w2_all[:], w2_words.bitcast(I32)[:, 0])
                 load_plane(w2_plane, w2_scales)
 
@@ -155,7 +155,7 @@ def tile_moe_pke_glu_silu_kernel(
         def gated(t):
             for s in range(PASSES):
                 first_layer(t, 3, s)
-            hidden[t] = work.tile([P, 2, P, 2], BF16, name="hidden", bufs=4)
+            hidden[t] = work.tile([P, 2, P, 2], BF16, name="hidden", bufs=TILES)
             nc.vector.tensor_tensor(hidden[t][:], gates[t][:], sums[(t, 3)][:].rearrange(order, u=2, d=2), MULT)
 
         packed = {}
@@ -168,13 +168,13 @@ def tile_moe_pke_glu_silu_kernel(
                 for u in range(2):
                     at = u * width + j * P
                     nc.tensor.transpose(bank[:, at : at + P], pairs[:, u * P : (u + 1) * P], ident[:])
-            rows = work.tile([P, 4 * C], BF16, name="rows", align_bytes=64)
+            rows = work.tile([P, 4 * C], BF16, name="rows", bufs=5, align_bytes=64)
             nc.scalar.copy(
                 rows[:, : 4 * width].bitcast(F32).rearrange("p (c u) -> p c u", u=2),
                 bank[:, : 2 * width].rearrange("p (u c) -> p c u", u=2),
             )
-            codes = work.tile([P, C], U32, name="codes", align_bytes=64)
-            scales = work.tile([P, C], U8, name="scales", align_bytes=64)
+            codes = work.tile([P, C], U32, name="codes", bufs=5, align_bytes=64)
+            scales = work.tile([P, C], U8, name="scales", bufs=5, align_bytes=64)
             nc.vector.quantize_mx(out=codes[:, :width].bitcast(FP8X4), scales=scales[:, :width], in_=rows[:, : 4 * width])
             packed[tiles] = (codes, scales)
 
@@ -194,7 +194,7 @@ def tile_moe_pke_glu_silu_kernel(
                 start=True,
                 stop=True,
             )
-            result = work.tile([P, C], F32, name="result", bufs=3)
+            result = work.tile([P, C], F32, name="result", bufs=5)
             copy_out(result[:, :width], bank[:, :width])
             if len(tiles) == 1:
                 nc.sync.dma_start(by_rank[:, e, tiles[0] % 2, :], result[:, :P])
@@ -215,13 +215,13 @@ def tile_moe_pke_glu_silu_kernel(
         gated(4)
         gated(5)
         turn((2, 3))
-        second_layer((0, 1), nc.scalar.copy)
         gated(6)
+        second_layer((0, 1), nc.scalar.copy)
         gated(7)
         turn((4, 5))
-        second_layer((2, 3), nc.scalar.copy)
+        second_layer((2, 3), nc.vector.tensor_copy)
         turn((6,))
         turn((7,))
-        second_layer((4, 5), nc.vector.tensor_copy)
-        second_layer((6,), nc.scalar.copy)
-        second_layer((7,), nc.vector.tensor_copy)
+        second_layer((4, 5), nc.scalar.copy)
+        second_layer((6,), nc.vector.tensor_copy)
+        second_layer((7,), nc.scalar.copy)

@@ -31,7 +31,7 @@ def tile_moe_pke_glu_silu_kernel(
     with ExitStack() as ctx:
         keep = ctx.enter_context(tc.tile_pool(name="keep", bufs=1))
         work = ctx.enter_context(tc.tile_pool(name="work", bufs=2))
-        psum = ctx.enter_context(tc.psum_pool(name="psum", bufs=8))
+        psum = ctx.enter_context(tc.psum_pool(name="psum", bufs=1))
 
         offsets = keep.tile([P, SLOTS // 16], U16, name="offsets")
         nc.sync.dma_start(offsets[:], offs)
@@ -43,6 +43,7 @@ def tile_moe_pke_glu_silu_kernel(
         w3_plane = keep.tile([P, E * PASSES * H], U8, name="w3_plane", align_bytes=64)
         ident = keep.tile([P, P], F32, name="ident")
 
+        nc.gpsimd.memset(xs_window[:].bitcast(I32), 0)
         make_identity(nc, ident[:])
 
         def clear(plane, zero):
@@ -61,19 +62,15 @@ def tile_moe_pke_glu_silu_kernel(
         w1_rows = w1_words.bitcast(I32)
         w3_rows = w3_words.bitcast(I32)
 
-        with tc.tile_pool(name="first_zero", bufs=1) as scratch:
-            zero = scratch.tile([P, 1], I32, name="zero")
-            nc.vector.memset(zero[:], 0)
-            nc.vector.memset(xs_window[:].bitcast(I32), 0)
-            xs_rows = x_scales.bitcast(I32)
-            for q in range(4):
-                nc.sync.dma_start(xs_window[32 * q : 32 * q + 8, :].bitcast(I32), xs_rows[:, 4 * q : 4 * q + 4, :])
-            clear(xs_pass1, zero)
+        w2_all = keep.tile([P, E * 2 * N], U8, name="w2_all", align_bytes=64)
+        load_rows(w2_all[:], w2_words.bitcast(I32)[:, 0])
+        xs_rows = x_scales.bitcast(I32)
+        for q in range(4):
+            queue = nc.sync if q < 2 else nc.scalar
+            queue.dma_start(xs_window[32 * q : 32 * q + 8, :].bitcast(I32), xs_rows[:, 4 * q : 4 * q + 4, :])
         first = ctx.enter_context(tc.tile_pool(name="first", bufs=1))
-        x0 = first.tile([P, T + E * 3 * N // 4], I32, name="x0", align_bytes=64, offset=0)[:, :T]
-        w1_pass0 = first.tile([P, E * ROW], U8, name="w1_pass0", align_bytes=64, offset=4 * T + E * 3 * N)
+        x0 = first.tile([P, T + E * N // 4], I32, name="x0", align_bytes=64, offset=0)[:, :T]
         nc.sync.dma_start(x0, x_rows[0])
-        load_rows(w1_pass0[:], w1_rows[:, 0])
         with tc.tile_pool(name="second_zero", bufs=1) as scratch:
             zero = scratch.tile([P, 1], I32, name="zero")
             nc.vector.memset(zero[:], 0)
@@ -81,6 +78,10 @@ def tile_moe_pke_glu_silu_kernel(
             load_plane(w1_plane, w1_scales)
             clear(w3_plane, zero)
         second = ctx.enter_context(tc.tile_pool(name="second", bufs=1))
+        w1_pass0 = []
+        for pair in range(2):
+            w1_pass0.append(second.tile([P, 2 * ROW], U8, name="w1_pass0_%d" % pair, align_bytes=64))
+            load_rows(w1_pass0[pair][:], w1_rows[2 * pair : 2 * pair + 2, 0])
         x1 = second.tile([P, T], I32, name="x1", align_bytes=64)
         nc.sync.dma_start(x1[:], x_rows[1])
         w1_pass1 = []
@@ -89,6 +90,7 @@ def tile_moe_pke_glu_silu_kernel(
             load_rows(w1_pass1[pair][:], w1_rows[2 * pair : 2 * pair + 2, 1])
         load_plane(w3_plane, w3_scales)
 
+        nc.vector.memset(xs_pass1[:].bitcast(I32), 0)
         warm_in = keep.tile([P, 1], F32, name="warm_in")
         warm_out = keep.tile([P, 1], F32, name="warm_out")
         nc.vector.memset(warm_in[:], 0.0)
@@ -108,23 +110,19 @@ def tile_moe_pke_glu_silu_kernel(
         for e in range(E):
             gather_words(0, x0, e)
 
-        w2_all = first.tile([P, E * 2 * N], U8, name="w2_all", align_bytes=64, offset=4 * T)
-        w2_plane = first.tile([P, E * N], U8, name="w2_plane", align_bytes=64, offset=4 * T + E * 2 * N)
+        w2_plane = first.tile([P, E * N], U8, name="w2_plane", align_bytes=64, offset=4 * T)
         nc.vector.memset(w2_plane[:].bitcast(I32), 0)
         w3_expert = []
         for e in range(E):
             w3_expert.append(first.tile([P, PASSES * ROW], U8, name="w3_%d" % e, align_bytes=64, offset=e * PASSES * ROW))
             load_rows(w3_expert[e][:], w3_rows[e])
             if e == 3:
-                load_rows(w2_all[:], w2_words.bitcast(I32)[:, 0])
                 load_plane(w2_plane, w2_scales)
 
         def weights(which, e, s):
             if which == 3:
                 return w3_expert[e][:, s * ROW : (s + 1) * ROW]
-            if s == 0:
-                return w1_pass0[:, e * ROW : (e + 1) * ROW]
-            return w1_pass1[e // 2][:, e % 2 * ROW : (e % 2 + 1) * ROW]
+            return (w1_pass0, w1_pass1)[s][e // 2][:, e % 2 * ROW : (e % 2 + 1) * ROW]
 
         planes = {1: w1_plane, 3: w3_plane}
         sums = {}
@@ -132,7 +130,7 @@ def tile_moe_pke_glu_silu_kernel(
         def first_layer(t, which, s):
             e, half = divmod(t, 2)
             if s == 0:
-                sums[(t, which)] = psum.tile([P, H], F32, name="bank")
+                sums[(t, which)] = psum.tile([P, H], F32, name="bank%d" % t)
             g = e * PASSES + s
             nc.tensor.matmul_mx(
                 out=sums[(t, which)][:],
@@ -160,16 +158,16 @@ def tile_moe_pke_glu_silu_kernel(
 
         packed = {}
 
-        def turn(tiles):
+        def turn(tiles, bank_number, copy_out):
             width = len(tiles) * P
-            bank = psum.tile([P, H], F32, name="bank")
+            bank = psum.tile([P, H], F32, name="bank%d" % bank_number)
             for j, t in enumerate(tiles):
                 pairs = hidden[t][:].rearrange("c u p d -> c (u p d)").bitcast(F32)
                 for u in range(2):
                     at = u * width + j * P
                     nc.tensor.transpose(bank[:, at : at + P], pairs[:, u * P : (u + 1) * P], ident[:])
             rows = work.tile([P, 4 * C], BF16, name="rows", bufs=5, align_bytes=64)
-            nc.scalar.copy(
+            copy_out(
                 rows[:, : 4 * width].bitcast(F32).rearrange("p (c u) -> p c u", u=2),
                 bank[:, : 2 * width].rearrange("p (u c) -> p c u", u=2),
             )
@@ -180,11 +178,11 @@ def tile_moe_pke_glu_silu_kernel(
 
         by_rank = out.rearrange("n (m e u) -> n e m u", m=RANKS, e=E)
 
-        def second_layer(tiles, copy_out):
+        def second_layer(tiles, bank_number, copy_out):
             width = len(tiles) * P
             e = tiles[0] // 2
             codes, scales = packed[tiles]
-            bank = psum.tile([P, H], F32, name="bank")
+            bank = psum.tile([P, H], F32, name="bank%d" % bank_number)
             nc.tensor.matmul_mx(
                 out=bank[:, :width],
                 lhsT=w2_all[:, e * 2 * N : (e + 1) * 2 * N].bitcast(FP4X4),
@@ -209,19 +207,10 @@ def tile_moe_pke_glu_silu_kernel(
             first_layer(t, 1, 1)
             silu(t)
 
-        for t in range(4):
+        for t in range(TILES):
             gated(t)
-        turn((0, 1))
-        gated(4)
-        gated(5)
-        turn((2, 3))
-        gated(6)
-        second_layer((0, 1), nc.scalar.copy)
-        gated(7)
-        turn((4, 5))
-        second_layer((2, 3), nc.vector.tensor_copy)
-        turn((6,))
-        turn((7,))
-        second_layer((4, 5), nc.scalar.copy)
-        second_layer((6,), nc.vector.tensor_copy)
-        second_layer((7,), nc.scalar.copy)
+        groups = [(0, 1), (2, 3), (4, 5), (6,), (7,)]
+        for tiles, bank_number in zip(groups, (4, 0, 1, 2, 3)):
+            turn(tiles, bank_number, nc.vector.tensor_copy if tiles == (6,) else nc.scalar.copy)
+        for tiles, bank_number in zip(groups, (5, 6, 7, 4, 0)):
+            second_layer(tiles, bank_number, nc.vector.tensor_copy if tiles == (4, 5) else nc.scalar.copy)

@@ -41,56 +41,54 @@ def tile_moe_pke_glu_silu_kernel(
         xs_pass1 = keep.tile([P, SLOTS], U8, name="xs_pass1", align_bytes=64)
         w1_plane = keep.tile([P, E * PASSES * H], U8, name="w1_plane", align_bytes=64)
         w3_plane = keep.tile([P, E * PASSES * H], U8, name="w3_plane", align_bytes=64)
+        w2_plane = keep.tile([P, E * N], U8, name="w2_plane", align_bytes=64)
         ident = keep.tile([P, P], F32, name="ident")
 
         nc.gpsimd.memset(xs_window[:].bitcast(I32), 0)
         make_identity(nc, ident[:])
+        for plane in (w1_plane, w3_plane, xs_pass1, w2_plane):
+            nc.vector.memset(plane[:].bitcast(I32), 0)
 
-        def clear(plane, zero):
-            words = plane[:].bitcast(I32)
-            nc.vector.tensor_copy(words, zero[:].to_broadcast(words.shape))
-
-        def load_plane(plane, scales):
+        def load_plane(queue, plane, scales):
             rows = scales.bitcast(I32).rearrange("e s (q r) i -> r q (e s) i", r=4)
             for r in range(4):
-                nc.sync.dma_start(plane[r:P:32, :].bitcast(I32).rearrange("q (g i) -> q g i", g=rows.shape[2]), rows[r])
+                queue.dma_start(plane[r:P:32, :].bitcast(I32).rearrange("q (g i) -> q g i", g=rows.shape[2]), rows[r])
 
-        def load_rows(tile, rows):
-            nc.sync.dma_start(tile.bitcast(I32).rearrange("p (g b) -> p g b", g=rows.shape[0]), rows.rearrange("g p b -> p g b"))
+        def load_rows(name, rows):
+            tile = keep.tile([P, rows.shape[0] * rows.shape[2] * 4], U8, name=name, align_bytes=64)
+            nc.sync.dma_start(tile[:].bitcast(I32).rearrange("p (g b) -> p g b", g=rows.shape[0]), rows.rearrange("g p b -> p g b"))
+            return tile
+
+        def load_window(s):
+            window = keep.tile([P, T], I32, name="x%d" % s, align_bytes=64)
+            nc.sync.dma_start(window[:], x_rows[s])
+            return window
 
         x_rows = x_words.rearrange("s p t r -> s p (t r)").bitcast(I32)
         w1_rows = w1_words.bitcast(I32)
         w3_rows = w3_words.bitcast(I32)
-
-        w2_all = keep.tile([P, E * 2 * N], U8, name="w2_all", align_bytes=64)
-        load_rows(w2_all[:], w2_words.bitcast(I32)[:, 0])
         xs_rows = x_scales.bitcast(I32)
+
+        w1_pairs = {}
+
+        def load_w1(s, pair):
+            w1_pairs[(s, pair)] = load_rows("w1_%d_%d" % (s, pair), w1_rows[2 * pair : 2 * pair + 2, s])
+
+        load_w1(0, 0)
         for q in range(4):
             queue = nc.sync if q < 2 else nc.scalar
             queue.dma_start(xs_window[32 * q : 32 * q + 8, :].bitcast(I32), xs_rows[:, 4 * q : 4 * q + 4, :])
-        first = ctx.enter_context(tc.tile_pool(name="first", bufs=1))
-        x0 = first.tile([P, T + E * N // 4], I32, name="x0", align_bytes=64, offset=0)[:, :T]
-        nc.sync.dma_start(x0, x_rows[0])
-        with tc.tile_pool(name="second_zero", bufs=1) as scratch:
-            zero = scratch.tile([P, 1], I32, name="zero")
-            nc.vector.memset(zero[:], 0)
-            nc.vector.memset(w1_plane[:].bitcast(I32), 0)
-            load_plane(w1_plane, w1_scales)
-            clear(w3_plane, zero)
-        second = ctx.enter_context(tc.tile_pool(name="second", bufs=1))
-        w1_pass0 = []
-        for pair in range(2):
-            w1_pass0.append(second.tile([P, 2 * ROW], U8, name="w1_pass0_%d" % pair, align_bytes=64))
-            load_rows(w1_pass0[pair][:], w1_rows[2 * pair : 2 * pair + 2, 0])
-        x1 = second.tile([P, T], I32, name="x1", align_bytes=64)
-        nc.sync.dma_start(x1[:], x_rows[1])
-        w1_pass1 = []
-        for pair in range(2):
-            w1_pass1.append(second.tile([P, 2 * ROW], U8, name="w1_pass1_%d" % pair, align_bytes=64))
-            load_rows(w1_pass1[pair][:], w1_rows[2 * pair : 2 * pair + 2, 1])
-        load_plane(w3_plane, w3_scales)
+        x0 = load_window(0)
+        load_plane(nc.scalar, w1_plane, w1_scales)
+        load_w1(0, 1)
+        x1 = load_window(1)
+        load_w1(1, 0)
+        load_w1(1, 1)
+        load_plane(nc.sync, w3_plane, w3_scales)
+        w3_expert = [load_rows("w3_%d" % e, w3_rows[e]) for e in range(E)]
+        w2_all = load_rows("w2_all", w2_words.bitcast(I32)[:, 0])
+        load_plane(nc.sync, w2_plane, w2_scales)
 
-        nc.vector.memset(xs_pass1[:].bitcast(I32), 0)
         warm_in = keep.tile([P, 1], F32, name="warm_in")
         warm_out = keep.tile([P, 1], F32, name="warm_out")
         nc.vector.memset(warm_in[:], 0.0)
@@ -104,25 +102,16 @@ def tile_moe_pke_glu_silu_kernel(
 
         def gather_words(s, window, e):
             tile = keep.tile([P, C], U32, name="xg%d_%d" % (s, e), align_bytes=64)
-            nc.vector.tensor_copy(tile[:], window.bitcast(U32).indirect(offsets[:, e * C // 16 : (e + 1) * C // 16]))
+            nc.vector.tensor_copy(tile[:], window[:].bitcast(U32).indirect(offsets[:, e * C // 16 : (e + 1) * C // 16]))
             gathered[(s, e)] = tile
 
         for e in range(E):
             gather_words(0, x0, e)
 
-        w2_plane = first.tile([P, E * N], U8, name="w2_plane", align_bytes=64, offset=4 * T)
-        nc.vector.memset(w2_plane[:].bitcast(I32), 0)
-        w3_expert = []
-        for e in range(E):
-            w3_expert.append(first.tile([P, PASSES * ROW], U8, name="w3_%d" % e, align_bytes=64, offset=e * PASSES * ROW))
-            load_rows(w3_expert[e][:], w3_rows[e])
-            if e == 3:
-                load_plane(w2_plane, w2_scales)
-
         def weights(which, e, s):
             if which == 3:
                 return w3_expert[e][:, s * ROW : (s + 1) * ROW]
-            return (w1_pass0, w1_pass1)[s][e // 2][:, e % 2 * ROW : (e % 2 + 1) * ROW]
+            return w1_pairs[(s, e // 2)][:, e % 2 * ROW : (e % 2 + 1) * ROW]
 
         planes = {1: w1_plane, 3: w3_plane}
         sums = {}
@@ -202,7 +191,7 @@ def tile_moe_pke_glu_silu_kernel(
         for t in range(TILES):
             first_layer(t, 1, 0)
         for e in range(E):
-            gather_words(1, x1[:], e)
+            gather_words(1, x1, e)
         for t in range(TILES):
             first_layer(t, 1, 1)
             silu(t)

@@ -36,67 +36,71 @@ def tile_moe_pke_glu_silu_kernel(
         offsets = keep.tile([P, SLOTS // 16], U16, name="offsets")
         nc.sync.dma_start(offsets[:], offs)
 
-        xs_window = keep.tile([P, T], U8, name="xs_window", align_bytes=64)
-        xs_slots = keep.tile([P, SLOTS], U8, name="xs_slots", align_bytes=64)
-        xs_pass1 = keep.tile([P, SLOTS], U8, name="xs_pass1", align_bytes=64)
+        xs_window = keep.tile([P, PASSES * T], U8, name="xs_window", align_bytes=64)
         w1_plane = keep.tile([P, E * PASSES * H], U8, name="w1_plane", align_bytes=64)
         w3_plane = keep.tile([P, E * PASSES * H], U8, name="w3_plane", align_bytes=64)
         w2_plane = keep.tile([P, E * N], U8, name="w2_plane", align_bytes=64)
         ident = keep.tile([P, P], F32, name="ident")
 
-        nc.gpsimd.memset(xs_window[:].bitcast(I32), 0)
+        nc.vector.memset(xs_window[:].bitcast(I32), 0)
         make_identity(nc, ident[:])
-        for plane in (w1_plane, w3_plane, xs_pass1, w2_plane):
-            nc.vector.memset(plane[:].bitcast(I32), 0)
+        with tc.tile_pool(name="zero", bufs=1) as scratch:
+            zero = scratch.tile([P, 1], I32, name="zero")
+            nc.vector.memset(zero[:], 0)
+            for plane in (w1_plane, w3_plane):
+                nc.vector.memset(plane[:].bitcast(I32), 0)
+            words = w2_plane[:].bitcast(I32)
+            nc.vector.tensor_copy(words, zero[:].to_broadcast(words.shape))
+        large = ctx.enter_context(tc.tile_pool(name="large", bufs=1))
 
-        def load_plane(queue, plane, scales):
+        def load_plane(plane, scales):
             rows = scales.bitcast(I32).rearrange("e s (q r) i -> r q (e s) i", r=4)
             for r in range(4):
-                queue.dma_start(plane[r:P:32, :].bitcast(I32).rearrange("q (g i) -> q g i", g=rows.shape[2]), rows[r])
+                nc.sync.dma_start(plane[r:P:32, :].bitcast(I32).rearrange("q (g i) -> q g i", g=rows.shape[2]), rows[r])
 
         def load_rows(name, rows):
-            tile = keep.tile([P, rows.shape[0] * rows.shape[2] * 4], U8, name=name, align_bytes=64)
+            tile = large.tile([P, rows.shape[0] * rows.shape[2] * 4], U8, name=name, align_bytes=64)
             nc.sync.dma_start(tile[:].bitcast(I32).rearrange("p (g b) -> p g b", g=rows.shape[0]), rows.rearrange("g p b -> p g b"))
             return tile
 
         def load_window(s):
-            window = keep.tile([P, T], I32, name="x%d" % s, align_bytes=64)
+            window = large.tile([P, T], I32, name="x%d" % s, align_bytes=64)
             nc.sync.dma_start(window[:], x_rows[s])
             return window
 
         x_rows = x_words.rearrange("s p t r -> s p (t r)").bitcast(I32)
         w1_rows = w1_words.bitcast(I32)
         w3_rows = w3_words.bitcast(I32)
-        xs_rows = x_scales.bitcast(I32)
+        xs_rows = x_scales.bitcast(I32).rearrange("s (q r) t -> r q s t", r=4)
 
         w1_pairs = {}
 
         def load_w1(s, pair):
             w1_pairs[(s, pair)] = load_rows("w1_%d_%d" % (s, pair), w1_rows[2 * pair : 2 * pair + 2, s])
 
-        load_w1(0, 0)
-        for q in range(4):
-            queue = nc.sync if q < 2 else nc.scalar
-            queue.dma_start(xs_window[32 * q : 32 * q + 8, :].bitcast(I32), xs_rows[:, 4 * q : 4 * q + 4, :])
+        for r in range(4):
+            nc.sync.dma_start(xs_window[r:P:32, :].bitcast(I32).rearrange("q (s t) -> q s t", s=PASSES), xs_rows[r])
+        load_plane(w1_plane, w1_scales)
+        load_plane(w3_plane, w3_scales)
         x0 = load_window(0)
-        load_plane(nc.scalar, w1_plane, w1_scales)
+        load_w1(0, 0)
         load_w1(0, 1)
         x1 = load_window(1)
         load_w1(1, 0)
         load_w1(1, 1)
-        load_plane(nc.sync, w3_plane, w3_scales)
         w3_expert = [load_rows("w3_%d" % e, w3_rows[e]) for e in range(E)]
         w2_all = load_rows("w2_all", w2_words.bitcast(I32)[:, 0])
-        load_plane(nc.sync, w2_plane, w2_scales)
+        load_plane(w2_plane, w2_scales)
 
         warm_in = keep.tile([P, 1], F32, name="warm_in")
         warm_out = keep.tile([P, 1], F32, name="warm_out")
         nc.vector.memset(warm_in[:], 0.0)
         nc.scalar.activation(warm_out[:], warm_in[:], SILU)
 
-        nc.vector.tensor_copy(xs_slots[:], xs_window[:].indirect(offsets[:]))
-        nc.scalar.dma_start(xs_pass1[0:100, :].bitcast(I32), xs_slots[4:104, :].bitcast(I32))
-        x_plane = [xs_slots, xs_pass1]
+        x_plane = []
+        for s in range(PASSES):
+            x_plane.append(keep.tile([P, SLOTS], U8, name="xs_slots%d" % s, align_bytes=64))
+            nc.vector.tensor_copy(x_plane[s][:], xs_window[:, s * T : (s + 1) * T].indirect(offsets[:]))
 
         gathered = {}
 

@@ -47,26 +47,22 @@ def tile_moe_pke_glu_silu_kernel(
         with tc.tile_pool(name="zero", bufs=1) as scratch:
             zero = scratch.tile([P, 1], I32, name="zero")
             nc.vector.memset(zero[:], 0)
-            for plane in (w1_plane, w3_plane):
-                nc.vector.memset(plane[:].bitcast(I32), 0)
+            nc.vector.memset(w1_plane[:].bitcast(I32), 0)
             words = w2_plane[:].bitcast(I32)
             nc.vector.tensor_copy(words, zero[:].to_broadcast(words.shape))
+        nc.vector.memset(w3_plane[:].bitcast(I32), 0)
         large = ctx.enter_context(tc.tile_pool(name="large", bufs=1))
+        later = ctx.enter_context(tc.tile_pool(name="later", bufs=1))
 
         def load_plane(plane, scales):
             rows = scales.bitcast(I32).rearrange("e s (q r) i -> r q (e s) i", r=4)
             for r in range(4):
                 nc.sync.dma_start(plane[r:P:32, :].bitcast(I32).rearrange("q (g i) -> q g i", g=rows.shape[2]), rows[r])
 
-        def load_rows(name, rows):
-            tile = large.tile([P, rows.shape[0] * rows.shape[2] * 4], U8, name=name, align_bytes=64)
+        def load_rows(pool, name, rows):
+            tile = pool.tile([P, rows.shape[0] * rows.shape[2] * 4], U8, name=name, align_bytes=64)
             nc.sync.dma_start(tile[:].bitcast(I32).rearrange("p (g b) -> p g b", g=rows.shape[0]), rows.rearrange("g p b -> p g b"))
             return tile
-
-        def load_window(s):
-            window = large.tile([P, T], I32, name="x%d" % s, align_bytes=64)
-            nc.sync.dma_start(window[:], x_rows[s])
-            return window
 
         x_rows = x_words.rearrange("s p t r -> s p (t r)").bitcast(I32)
         w1_rows = w1_words.bitcast(I32)
@@ -75,21 +71,23 @@ def tile_moe_pke_glu_silu_kernel(
 
         w1_pairs = {}
 
-        def load_w1(s, pair):
-            w1_pairs[(s, pair)] = load_rows("w1_%d_%d" % (s, pair), w1_rows[2 * pair : 2 * pair + 2, s])
+        def load_w1(pool, s, pair):
+            w1_pairs[(s, pair)] = load_rows(pool, "w1_%d_%d" % (s, pair), w1_rows[2 * pair : 2 * pair + 2, s])
 
+        load_w1(keep, 0, 0)
         for r in range(4):
             nc.sync.dma_start(xs_window[r:P:32, :].bitcast(I32).rearrange("q (s t) -> q s t", s=PASSES), xs_rows[r])
         load_plane(w1_plane, w1_scales)
+        x0 = large.tile([P, T + SLOTS // 8], I32, name="x0", align_bytes=64, offset=0)[:, :T]
+        nc.sync.dma_start(x0, x_rows[0])
+        load_w1(later, 0, 1)
+        x1 = later.tile([P, T], I32, name="x1", align_bytes=64)[:]
+        nc.sync.dma_start(x1, x_rows[1])
+        load_w1(later, 1, 0)
+        load_w1(later, 1, 1)
         load_plane(w3_plane, w3_scales)
-        x0 = load_window(0)
-        load_w1(0, 0)
-        load_w1(0, 1)
-        x1 = load_window(1)
-        load_w1(1, 0)
-        load_w1(1, 1)
-        w3_expert = [load_rows("w3_%d" % e, w3_rows[e]) for e in range(E)]
-        w2_all = load_rows("w2_all", w2_words.bitcast(I32)[:, 0])
+        w3_expert = [load_rows(later, "w3_%d" % e, w3_rows[e]) for e in range(E)]
+        w2_all = load_rows(later, "w2_all", w2_words.bitcast(I32)[:, 0])
         load_plane(w2_plane, w2_scales)
 
         warm_in = keep.tile([P, 1], F32, name="warm_in")
@@ -97,20 +95,27 @@ def tile_moe_pke_glu_silu_kernel(
         nc.vector.memset(warm_in[:], 0.0)
         nc.scalar.activation(warm_out[:], warm_in[:], SILU)
 
-        x_plane = []
-        for s in range(PASSES):
-            x_plane.append(keep.tile([P, SLOTS], U8, name="xs_slots%d" % s, align_bytes=64))
-            nc.vector.tensor_copy(x_plane[s][:], xs_window[:, s * T : (s + 1) * T].indirect(offsets[:]))
+        half = SLOTS // 2
+        x_plane = {}
+
+        def gather_scales(s, first, count, tile):
+            nc.vector.tensor_copy(tile[:], xs_window[:, s * T : (s + 1) * T].indirect(offsets[:, first // 16 : (first + count) // 16]))
+            for t in range(first // P, (first + count) // P):
+                x_plane[(s, t)] = tile[:, t * P - first : (t + 1) * P - first]
+
+        gather_scales(0, 0, SLOTS, keep.tile([P, SLOTS], U8, name="xs_pass0", align_bytes=64))
+        gather_scales(1, 0, half, keep.tile([P, half], U8, name="xs_pass1_low", align_bytes=64))
 
         gathered = {}
 
         def gather_words(s, window, e):
             tile = keep.tile([P, C], U32, name="xg%d_%d" % (s, e), align_bytes=64)
-            nc.vector.tensor_copy(tile[:], window[:].bitcast(U32).indirect(offsets[:, e * C // 16 : (e + 1) * C // 16]))
+            nc.vector.tensor_copy(tile[:], window.bitcast(U32).indirect(offsets[:, e * C // 16 : (e + 1) * C // 16]))
             gathered[(s, e)] = tile
 
         for e in range(E):
             gather_words(0, x0, e)
+        gather_scales(1, half, half, large.tile([P, half], U8, name="xs_pass1_high", align_bytes=64, offset=4 * T))
 
         def weights(which, e, s):
             if which == 3:
@@ -128,7 +133,7 @@ def tile_moe_pke_glu_silu_kernel(
             nc.tensor.matmul_mx(
                 out=sums[(t, which)][:],
                 lhsT=gathered[(s, e)][:, half * P : (half + 1) * P].bitcast(FP8X4),
-                lhsT_scale=x_plane[s][:, t * P : (t + 1) * P],
+                lhsT_scale=x_plane[(s, t)],
                 rhs=weights(which, e, s).bitcast(FP4X4),
                 rhs_scale=planes[which][:, g * H : (g + 1) * H],
                 start=(s == 0),

@@ -36,9 +36,11 @@ def tile_moe_pke_glu_silu_kernel(
         offsets = keep.tile([P, SLOTS // 16], U16, name="offsets")
         nc.sync.dma_start(offsets[:], offs)
 
-        xs_window = keep.tile([P, PASSES * T], U8, name="xs_window", align_bytes=64)
+        xs_window = keep.tile([P, T], U8, name="xs_window", align_bytes=64)
+        xs_slots = keep.tile([P, SLOTS], U8, name="xs_slots", align_bytes=64)
+        xs_pass1 = keep.tile([P, SLOTS], U8, name="xs_pass1", align_bytes=64)
         w1_plane = keep.tile([P, E * PASSES * H], U8, name="w1_plane", align_bytes=64)
-        w3_plane = keep.tile([P, E * PASSES * H], U8, name="w3_plane", align_bytes=64)
+        w3_planes = [keep.tile([P, 2 * PASSES * H], U8, name="w3_plane%d" % pair, align_bytes=64) for pair in range(2)]
         w2_plane = keep.tile([P, E * N], U8, name="w2_plane", align_bytes=64)
         ident = keep.tile([P, P], F32, name="ident")
 
@@ -47,15 +49,14 @@ def tile_moe_pke_glu_silu_kernel(
         with tc.tile_pool(name="zero", bufs=1) as scratch:
             zero = scratch.tile([P, 1], I32, name="zero")
             nc.vector.memset(zero[:], 0)
-            nc.vector.memset(w1_plane[:].bitcast(I32), 0)
-            words = w2_plane[:].bitcast(I32)
+            words = xs_pass1[:].bitcast(I32)
             nc.vector.tensor_copy(words, zero[:].to_broadcast(words.shape))
-        nc.vector.memset(w3_plane[:].bitcast(I32), 0)
-        large = ctx.enter_context(tc.tile_pool(name="large", bufs=1))
+        for plane in [w1_plane] + w3_planes + [w2_plane]:
+            nc.vector.memset(plane[:].bitcast(I32), 0)
         later = ctx.enter_context(tc.tile_pool(name="later", bufs=1))
 
         def load_plane(plane, scales):
-            rows = scales.bitcast(I32).rearrange("e s (q r) i -> r q (e s) i", r=4)
+            rows = scales.rearrange("e s (q r) i -> r q (e s) i", r=4)
             for r in range(4):
                 nc.sync.dma_start(plane[r:P:32, :].bitcast(I32).rearrange("q (g i) -> q g i", g=rows.shape[2]), rows[r])
 
@@ -67,7 +68,7 @@ def tile_moe_pke_glu_silu_kernel(
         x_rows = x_words.rearrange("s p t r -> s p (t r)").bitcast(I32)
         w1_rows = w1_words.bitcast(I32)
         w3_rows = w3_words.bitcast(I32)
-        xs_rows = x_scales.bitcast(I32).rearrange("s (q r) t -> r q s t", r=4)
+        xs_rows = x_scales.bitcast(I32)
 
         w1_pairs = {}
 
@@ -75,37 +76,32 @@ def tile_moe_pke_glu_silu_kernel(
             w1_pairs[(s, pair)] = load_rows(pool, "w1_%d_%d" % (s, pair), w1_rows[2 * pair : 2 * pair + 2, s])
 
         load_w1(keep, 0, 0)
-        for r in range(4):
-            nc.sync.dma_start(xs_window[r:P:32, :].bitcast(I32).rearrange("q (s t) -> q s t", s=PASSES), xs_rows[r])
-        load_plane(w1_plane, w1_scales)
-        x0 = large.tile([P, T + SLOTS // 8], I32, name="x0", align_bytes=64, offset=0)[:, :T]
+        for q in range(4):
+            nc.sync.dma_start(xs_window[32 * q : 32 * q + 8, :].bitcast(I32), xs_rows[:, 4 * q : 4 * q + 4, :])
+        nc.vector.tensor_copy(xs_slots[:], xs_window[:].indirect(offsets[:]))
+        x0 = later.tile([P, T], I32, name="x0", align_bytes=64)[:]
         nc.sync.dma_start(x0, x_rows[0])
+        load_plane(w1_plane, w1_scales.bitcast(I32))
         load_w1(later, 0, 1)
         x1 = later.tile([P, T], I32, name="x1", align_bytes=64)[:]
         nc.sync.dma_start(x1, x_rows[1])
+        nc.sync.dma_start(xs_pass1[0:100, :].bitcast(I32), xs_slots[4:104, :].bitcast(I32))
         load_w1(later, 1, 0)
         load_w1(later, 1, 1)
-        load_plane(w3_plane, w3_scales)
-        w3_expert = [load_rows(later, "w3_%d" % e, w3_rows[e]) for e in range(E)]
+        w3_expert = []
+        for pair in range(2):
+            load_plane(w3_planes[pair], w3_scales.bitcast(I32)[2 * pair : 2 * pair + 2])
+            for e in (2 * pair, 2 * pair + 1):
+                w3_expert.append(load_rows(later, "w3_%d" % e, w3_rows[e]))
         w2_all = load_rows(later, "w2_all", w2_words.bitcast(I32)[:, 0])
-        load_plane(w2_plane, w2_scales)
+        load_plane(w2_plane, w2_scales.bitcast(I32))
 
         warm_in = keep.tile([P, 1], F32, name="warm_in")
         warm_out = keep.tile([P, 1], F32, name="warm_out")
         nc.vector.memset(warm_in[:], 0.0)
         nc.scalar.activation(warm_out[:], warm_in[:], SILU)
 
-        half = SLOTS // 2
-        x_plane = {}
-
-        def gather_scales(s, first, count, tile):
-            nc.vector.tensor_copy(tile[:], xs_window[:, s * T : (s + 1) * T].indirect(offsets[:, first // 16 : (first + count) // 16]))
-            for t in range(first // P, (first + count) // P):
-                x_plane[(s, t)] = tile[:, t * P - first : (t + 1) * P - first]
-
-        gather_scales(0, 0, SLOTS, keep.tile([P, SLOTS], U8, name="xs_pass0", align_bytes=64))
-        gather_scales(1, 0, half, keep.tile([P, half], U8, name="xs_pass1_low", align_bytes=64))
-
+        x_plane = [xs_slots, xs_pass1]
         gathered = {}
 
         def gather_words(s, window, e):
@@ -115,27 +111,31 @@ def tile_moe_pke_glu_silu_kernel(
 
         for e in range(E):
             gather_words(0, x0, e)
-        gather_scales(1, half, half, large.tile([P, half], U8, name="xs_pass1_high", align_bytes=64, offset=4 * T))
 
         def weights(which, e, s):
             if which == 3:
                 return w3_expert[e][:, s * ROW : (s + 1) * ROW]
             return w1_pairs[(s, e // 2)][:, e % 2 * ROW : (e % 2 + 1) * ROW]
 
-        planes = {1: w1_plane, 3: w3_plane}
+        def weight_scales(which, e, s):
+            if which == 3:
+                g = e % 2 * PASSES + s
+                return w3_planes[e // 2][:, g * H : (g + 1) * H]
+            g = e * PASSES + s
+            return w1_plane[:, g * H : (g + 1) * H]
+
         sums = {}
 
         def first_layer(t, which, s):
             e, half = divmod(t, 2)
             if s == 0:
                 sums[(t, which)] = psum.tile([P, H], F32, name="bank%d" % t)
-            g = e * PASSES + s
             nc.tensor.matmul_mx(
                 out=sums[(t, which)][:],
                 lhsT=gathered[(s, e)][:, half * P : (half + 1) * P].bitcast(FP8X4),
-                lhsT_scale=x_plane[(s, t)],
+                lhsT_scale=x_plane[s][:, t * P : (t + 1) * P],
                 rhs=weights(which, e, s).bitcast(FP4X4),
-                rhs_scale=planes[which][:, g * H : (g + 1) * H],
+                rhs_scale=weight_scales(which, e, s),
                 start=(s == 0),
                 stop=(s == PASSES - 1),
             )
@@ -208,7 +208,7 @@ def tile_moe_pke_glu_silu_kernel(
         for t in range(TILES):
             gated(t)
         groups = [(0, 1), (2, 3), (4, 5), (6,), (7,)]
-        for tiles, bank_number in zip(groups, (4, 0, 1, 2, 3)):
+        for tiles, bank_number in zip(groups, (4, 5, 0, 1, 2)):
             turn(tiles, bank_number, nc.vector.tensor_copy if tiles == (6,) else nc.scalar.copy)
-        for tiles, bank_number in zip(groups, (5, 6, 7, 4, 0)):
-            second_layer(tiles, bank_number, nc.vector.tensor_copy if tiles == (4, 5) else nc.scalar.copy)
+        for tiles, bank_number in zip(groups, (3, 6, 7, 4, 5)):
+            second_layer(tiles, bank_number, nc.vector.tensor_copy if len(tiles) == 1 else nc.scalar.copy)

@@ -44,11 +44,11 @@ def tile_moe_pke_glu_silu_kernel(
         w2_plane = keep.tile([P, E * N], U8, name="w2_plane", align_bytes=64)
         ident = keep.tile([P, P], F32, name="ident")
 
-        nc.vector.memset(xs_window[:].bitcast(I32), 0)
         make_identity(nc, ident[:])
         with tc.tile_pool(name="zero", bufs=1) as scratch:
             zero = scratch.tile([P, 1], I32, name="zero")
             nc.vector.memset(zero[:], 0)
+            nc.vector.memset(xs_window[:].bitcast(I32), 0)
             words = xs_pass1[:].bitcast(I32)
             nc.vector.tensor_copy(words, zero[:].to_broadcast(words.shape))
         for plane in [w1_plane] + w3_planes + [w2_plane]:
@@ -68,7 +68,7 @@ def tile_moe_pke_glu_silu_kernel(
         x_rows = x_words.rearrange("s p t r -> s p (t r)").bitcast(I32)
         w1_rows = w1_words.bitcast(I32)
         w3_rows = w3_words.bitcast(I32)
-        xs_rows = x_scales.bitcast(I32)
+        xs_rows = x_scales.bitcast(I32).rearrange("s (q r) t -> r q s t", r=4)
 
         w1_pairs = {}
 
@@ -76,16 +76,16 @@ def tile_moe_pke_glu_silu_kernel(
             w1_pairs[(s, pair)] = load_rows(pool, "w1_%d_%d" % (s, pair), w1_rows[2 * pair : 2 * pair + 2, s])
 
         load_w1(keep, 0, 0)
-        for q in range(4):
-            nc.sync.dma_start(xs_window[32 * q : 32 * q + 8, :].bitcast(I32), xs_rows[:, 4 * q : 4 * q + 4, :])
+        for r in range(4):
+            nc.sync.dma_start(xs_window[r:P:16, :].bitcast(I32), xs_rows[r])
         nc.vector.tensor_copy(xs_slots[:], xs_window[:].indirect(offsets[:]))
         x0 = later.tile([P, T], I32, name="x0", align_bytes=64)[:]
         nc.sync.dma_start(x0, x_rows[0])
         load_plane(w1_plane, w1_scales.bitcast(I32))
-        load_w1(later, 0, 1)
         x1 = later.tile([P, T], I32, name="x1", align_bytes=64)[:]
         nc.sync.dma_start(x1, x_rows[1])
-        nc.sync.dma_start(xs_pass1[0:100, :].bitcast(I32), xs_slots[4:104, :].bitcast(I32))
+        load_w1(later, 0, 1)
+        nc.sync.dma_start(xs_pass1[0:100, :].bitcast(I32), xs_slots[16:116, :].bitcast(I32))
         load_w1(later, 1, 0)
         load_w1(later, 1, 1)
         w3_expert = []
@@ -95,11 +95,6 @@ def tile_moe_pke_glu_silu_kernel(
                 w3_expert.append(load_rows(later, "w3_%d" % e, w3_rows[e]))
         w2_all = load_rows(later, "w2_all", w2_words.bitcast(I32)[:, 0])
         load_plane(w2_plane, w2_scales.bitcast(I32))
-
-        warm_in = keep.tile([P, 1], F32, name="warm_in")
-        warm_out = keep.tile([P, 1], F32, name="warm_out")
-        nc.vector.memset(warm_in[:], 0.0)
-        nc.scalar.activation(warm_out[:], warm_in[:], SILU)
 
         x_plane = [xs_slots, xs_pass1]
         gathered = {}

@@ -21,7 +21,10 @@ FP8X4 = mybir.dt.float8_e4m3fn_x4
 FP4X4 = mybir.dt.float4_e2m1fn_x4
 SILU = mybir.ActivationFunctionType.Silu
 MULT = mybir.AluOpType.mult
+
 ROW = 2 * H
+SHIFT = 16
+LIVE_SPAN = 100
 
 
 def tile_moe_pke_glu_silu_kernel(
@@ -30,7 +33,6 @@ def tile_moe_pke_glu_silu_kernel(
     nc = tc.nc
     with ExitStack() as ctx:
         keep = ctx.enter_context(tc.tile_pool(name="keep", bufs=1))
-        work = ctx.enter_context(tc.tile_pool(name="work", bufs=2))
         psum = ctx.enter_context(tc.psum_pool(name="psum", bufs=1))
 
         offsets = keep.tile([P, SLOTS // 16], U16, name="offsets")
@@ -49,8 +51,8 @@ def tile_moe_pke_glu_silu_kernel(
             zero = scratch.tile([P, 1], I32, name="zero")
             nc.vector.memset(zero[:], 0)
             nc.vector.memset(xs_window[:].bitcast(I32), 0)
-            words = xs_pass1[:].bitcast(I32)
-            nc.vector.tensor_copy(words, zero[:].to_broadcast(words.shape))
+            cleared = xs_pass1[:].bitcast(I32)
+            nc.vector.tensor_copy(cleared, zero[:].to_broadcast(cleared.shape))
         for plane in [w1_plane] + w3_planes + [w2_plane]:
             nc.vector.memset(plane[:].bitcast(I32), 0)
         later = ctx.enter_context(tc.tile_pool(name="later", bufs=1))
@@ -66,71 +68,74 @@ def tile_moe_pke_glu_silu_kernel(
             return tile
 
         x_rows = x_words.rearrange("s p t r -> s p (t r)").bitcast(I32)
-        w1_rows = w1_words.bitcast(I32)
-        w3_rows = w3_words.bitcast(I32)
         xs_rows = x_scales.bitcast(I32).rearrange("s (q r) t -> r q s t", r=4)
+        word_rows = {1: w1_words.bitcast(I32), 3: w3_words.bitcast(I32)}
+        weights = {}
+        windows = {}
 
-        w1_pairs = {}
+        def load_window(s):
+            windows[s] = later.tile([P, T], I32, name="x%d" % s, align_bytes=64)
+            nc.sync.dma_start(windows[s][:], x_rows[s])
 
-        def load_w1(pool, s, pair):
-            w1_pairs[(s, pair)] = load_rows(pool, "w1_%d_%d" % (s, pair), w1_rows[2 * pair : 2 * pair + 2, s])
+        def load_experts(pool, which, first, count, s):
+            tile = load_rows(pool, "w%d_%d_%d" % (which, first, s), word_rows[which][first : first + count, s])
+            for j in range(count):
+                weights[(which, first + j, s)] = tile[:, j * ROW : (j + 1) * ROW]
 
-        load_w1(keep, 0, 0)
+        def load_both_passes(which, e):
+            tile = load_rows(later, "w%d_%d" % (which, e), word_rows[which][e])
+            for s in range(PASSES):
+                weights[(which, e, s)] = tile[:, s * ROW : (s + 1) * ROW]
+
+        load_experts(keep, 1, 0, 2, 0)
         for r in range(4):
-            nc.sync.dma_start(xs_window[r:P:16, :].bitcast(I32), xs_rows[r])
+            nc.sync.dma_start(xs_window[r:P:SHIFT, :].bitcast(I32), xs_rows[r])
         nc.vector.tensor_copy(xs_slots[:], xs_window[:].indirect(offsets[:]))
-        x0 = later.tile([P, T], I32, name="x0", align_bytes=64)[:]
-        nc.sync.dma_start(x0, x_rows[0])
+        load_window(0)
         load_plane(w1_plane, w1_scales.bitcast(I32))
-        x1 = later.tile([P, T], I32, name="x1", align_bytes=64)[:]
-        nc.sync.dma_start(x1, x_rows[1])
-        load_w1(later, 0, 1)
-        nc.sync.dma_start(xs_pass1[0:100, :].bitcast(I32), xs_slots[16:116, :].bitcast(I32))
-        load_w1(later, 1, 0)
-        load_w1(later, 1, 1)
-        w3_expert = []
+        load_experts(later, 1, 2, 1, 0)
+        load_window(1)
+        load_experts(later, 1, 3, 1, 0)
+        nc.sync.dma_start(xs_pass1[0:LIVE_SPAN, :].bitcast(I32), xs_slots[SHIFT : SHIFT + LIVE_SPAN, :].bitcast(I32))
+        load_experts(later, 1, 0, 1, 1)
+        load_experts(later, 1, 1, 1, 1)
+        load_experts(later, 1, 2, 2, 1)
         for pair in range(2):
             load_plane(w3_planes[pair], w3_scales.bitcast(I32)[2 * pair : 2 * pair + 2])
-            for e in (2 * pair, 2 * pair + 1):
-                w3_expert.append(load_rows(later, "w3_%d" % e, w3_rows[e]))
+            for s in range(PASSES):
+                load_experts(later, 3, 2 * pair, 1, s)
+            load_both_passes(3, 2 * pair + 1)
         w2_all = load_rows(later, "w2_all", w2_words.bitcast(I32)[:, 0])
         load_plane(w2_plane, w2_scales.bitcast(I32))
 
         x_plane = [xs_slots, xs_pass1]
         gathered = {}
 
-        def gather_words(s, window, e):
-            tile = keep.tile([P, C], U32, name="xg%d_%d" % (s, e), align_bytes=64)
-            nc.vector.tensor_copy(tile[:], window.bitcast(U32).indirect(offsets[:, e * C // 16 : (e + 1) * C // 16]))
-            gathered[(s, e)] = tile
+        def gather_words(s):
+            for e in range(E):
+                gathered[(s, e)] = keep.tile([P, C], U32, name="xg%d_%d" % (s, e), align_bytes=64)
+                picks = offsets[:, e * C // 16 : (e + 1) * C // 16]
+                nc.vector.tensor_copy(gathered[(s, e)][:], windows[s][:].bitcast(U32).indirect(picks))
 
-        for e in range(E):
-            gather_words(0, x0, e)
-
-        def weights(which, e, s):
-            if which == 3:
-                return w3_expert[e][:, s * ROW : (s + 1) * ROW]
-            return w1_pairs[(s, e // 2)][:, e % 2 * ROW : (e % 2 + 1) * ROW]
-
-        def weight_scales(which, e, s):
-            if which == 3:
-                g = e % 2 * PASSES + s
-                return w3_planes[e // 2][:, g * H : (g + 1) * H]
-            g = e * PASSES + s
-            return w1_plane[:, g * H : (g + 1) * H]
+        def bank(number):
+            return psum.tile([P, H], F32, name="bank%d" % number)
 
         sums = {}
 
         def first_layer(t, which, s):
-            e, half = divmod(t, 2)
+            e, rank = divmod(t, RANKS)
             if s == 0:
-                sums[(t, which)] = psum.tile([P, H], F32, name="bank%d" % t)
+                sums[(t, which)] = bank(t)
+            if which == 1:
+                plane, g = w1_plane, e * PASSES + s
+            else:
+                plane, g = w3_planes[e // 2], e % 2 * PASSES + s
             nc.tensor.matmul_mx(
                 out=sums[(t, which)][:],
-                lhsT=gathered[(s, e)][:, half * P : (half + 1) * P].bitcast(FP8X4),
+                lhsT=gathered[(s, e)][:, rank * P : (rank + 1) * P].bitcast(FP8X4),
                 lhsT_scale=x_plane[s][:, t * P : (t + 1) * P],
-                rhs=weights(which, e, s).bitcast(FP4X4),
-                rhs_scale=weight_scales(which, e, s),
+                rhs=weights[(which, e, s)].bitcast(FP4X4),
+                rhs_scale=plane[:, g * H : (g + 1) * H],
                 start=(s == 0),
                 stop=(s == PASSES - 1),
             )
@@ -140,70 +145,75 @@ def tile_moe_pke_glu_silu_kernel(
         hidden = {}
 
         def silu(t):
-            gates[t] = work.tile([P, 2, P, 2], F32, name="gate", bufs=TILES)
+            gates[t] = keep.tile([P, 2, P, 2], F32, name="gate%d" % t)
             nc.scalar.activation(gates[t][:], sums[(t, 1)][:].rearrange(order, u=2, d=2), SILU)
 
-        def gated(t):
-            for s in range(PASSES):
-                first_layer(t, 3, s)
-            hidden[t] = work.tile([P, 2, P, 2], BF16, name="hidden", bufs=TILES)
+        def gate(t):
+            hidden[t] = keep.tile([P, 2, P, 2], BF16, name="hidden%d" % t)
             nc.vector.tensor_tensor(hidden[t][:], gates[t][:], sums[(t, 3)][:].rearrange(order, u=2, d=2), MULT)
 
         packed = {}
 
         def turn(tiles, bank_number, copy_out):
             width = len(tiles) * P
-            bank = psum.tile([P, H], F32, name="bank%d" % bank_number)
+            turned = bank(bank_number)
             for j, t in enumerate(tiles):
                 pairs = hidden[t][:].rearrange("c u p d -> c (u p d)").bitcast(F32)
                 for u in range(2):
                     at = u * width + j * P
-                    nc.tensor.transpose(bank[:, at : at + P], pairs[:, u * P : (u + 1) * P], ident[:])
-            rows = work.tile([P, 4 * C], BF16, name="rows", bufs=5, align_bytes=64)
+                    nc.tensor.transpose(turned[:, at : at + P], pairs[:, u * P : (u + 1) * P], ident[:])
+            rows = keep.tile([P, 4 * width], BF16, name="rows%d" % tiles[0], align_bytes=64)
             copy_out(
-                rows[:, : 4 * width].bitcast(F32).rearrange("p (c u) -> p c u", u=2),
-                bank[:, : 2 * width].rearrange("p (u c) -> p c u", u=2),
+                rows[:].bitcast(F32).rearrange("p (c u) -> p c u", u=2),
+                turned[:, : 2 * width].rearrange("p (u c) -> p c u", u=2),
             )
-            codes = work.tile([P, C], U32, name="codes", bufs=5, align_bytes=64)
-            scales = work.tile([P, C], U8, name="scales", bufs=5, align_bytes=64)
-            nc.vector.quantize_mx(out=codes[:, :width].bitcast(FP8X4), scales=scales[:, :width], in_=rows[:, : 4 * width])
+            codes = keep.tile([P, width], U32, name="codes%d" % tiles[0], align_bytes=64)
+            scales = keep.tile([P, width], U8, name="scales%d" % tiles[0], align_bytes=64)
+            nc.vector.quantize_mx(out=codes[:].bitcast(FP8X4), scales=scales[:], in_=rows[:])
             packed[tiles] = (codes, scales)
 
         by_rank = out.rearrange("n (m e u) -> n e m u", m=RANKS, e=E)
 
         def second_layer(tiles, bank_number, copy_out):
             width = len(tiles) * P
-            e = tiles[0] // 2
+            e = tiles[0] // RANKS
             codes, scales = packed[tiles]
-            bank = psum.tile([P, H], F32, name="bank%d" % bank_number)
+            product = bank(bank_number)
             nc.tensor.matmul_mx(
-                out=bank[:, :width],
+                out=product[:, :width],
                 lhsT=w2_all[:, e * 2 * N : (e + 1) * 2 * N].bitcast(FP4X4),
                 lhsT_scale=w2_plane[:, e * N : (e + 1) * N],
-                rhs=codes[:, :width].bitcast(FP8X4),
-                rhs_scale=scales[:, :width],
+                rhs=codes[:].bitcast(FP8X4),
+                rhs_scale=scales[:],
                 start=True,
                 stop=True,
             )
-            result = work.tile([P, C], F32, name="result", bufs=5)
-            copy_out(result[:, :width], bank[:, :width])
+            result = keep.tile([P, width], F32, name="result%d" % tiles[0])
+            copy_out(result[:], product[:, :width])
             if len(tiles) == 1:
-                nc.sync.dma_start(by_rank[:, e, tiles[0] % 2, :], result[:, :P])
+                nc.sync.dma_start(by_rank[:, e, tiles[0] % RANKS, :], result[:])
             else:
                 nc.sync.dma_start(by_rank[:, e], result[:].rearrange("n (m u) -> n m u", u=P))
 
+        gather_words(0)
         for t in range(TILES):
             first_layer(t, 1, 0)
-        for e in range(E):
-            gather_words(1, x1, e)
+        gather_words(1)
         for t in range(TILES):
             first_layer(t, 1, 1)
             silu(t)
-
-        for t in range(TILES):
-            gated(t)
+        for e in range(E):
+            tiles = (RANKS * e, RANKS * e + 1)
+            if e % 2 == 0:
+                steps = [(t, s) for s in range(PASSES) for t in tiles]
+            else:
+                steps = [(t, s) for t in tiles for s in range(PASSES)]
+            for t, s in steps:
+                first_layer(t, 3, s)
+                if s == PASSES - 1:
+                    gate(t)
         groups = [(0, 1), (2, 3), (4, 5), (6,), (7,)]
         for tiles, bank_number in zip(groups, (4, 5, 0, 1, 2)):
-            turn(tiles, bank_number, nc.vector.tensor_copy if tiles == (6,) else nc.scalar.copy)
+            turn(tiles, bank_number, nc.vector.tensor_copy if tiles == (2, 3) else nc.scalar.copy)
         for tiles, bank_number in zip(groups, (3, 6, 7, 4, 5)):
             second_layer(tiles, bank_number, nc.vector.tensor_copy if len(tiles) == 1 else nc.scalar.copy)

@@ -36,7 +36,6 @@ def tile_moe_pke_glu_silu_kernel(
         psum = ctx.enter_context(tc.psum_pool(name="psum", bufs=1))
 
         offsets = keep.tile([P, SLOTS // 16], U16, name="offsets")
-        nc.sync.dma_start(offsets[:], offs)
 
         xs_window = keep.tile([P, T], U8, name="xs_window", align_bytes=64)
         xs_slots = keep.tile([P, SLOTS], U8, name="xs_slots", align_bytes=64)
@@ -88,6 +87,7 @@ def tile_moe_pke_glu_silu_kernel(
                 weights[(which, e, s)] = tile[:, s * ROW : (s + 1) * ROW]
 
         load_experts(keep, 1, 0, 2, 0)
+        nc.sync.dma_start(offsets[:], offs)
         for r in range(4):
             nc.sync.dma_start(xs_window[r:P:SHIFT, :].bitcast(I32), xs_rows[r])
         nc.vector.tensor_copy(xs_slots[:], xs_window[:].indirect(offsets[:]))
@@ -173,6 +173,7 @@ def tile_moe_pke_glu_silu_kernel(
             packed[tiles] = (codes, scales)
 
         by_rank = out.rearrange("n (m e u) -> n e m u", m=RANKS, e=E)
+        last_two = keep.tile([P, RANKS, 2 * P], F32, name="last_two")
 
         def second_layer(tiles, bank_number, copy_out):
             width = len(tiles) * P
@@ -188,12 +189,17 @@ def tile_moe_pke_glu_silu_kernel(
                 start=True,
                 stop=True,
             )
-            result = keep.tile([P, width], F32, name="result%d" % tiles[0])
-            copy_out(result[:], product[:, :width])
-            if len(tiles) == 1:
-                nc.sync.dma_start(by_rank[:, e, tiles[0] % RANKS, :], result[:])
+            if e < 2:
+                result = keep.tile([P, RANKS, P], F32, name="result%d" % e)
+                copy_out(result[:], product[:, :C].rearrange("n (m u) -> n m u", u=P))
+                nc.sync.dma_start(by_rank[:, e], result[:])
+            elif e == 2:
+                copy_out(last_two[:, :, :P], product[:, :C].rearrange("n (m u) -> n m u", u=P))
             else:
-                nc.sync.dma_start(by_rank[:, e], result[:].rearrange("n (m u) -> n m u", u=P))
+                rank = tiles[0] % RANKS
+                copy_out(last_two[:, rank, P:], product[:, :P])
+                at = rank * E * P + 2 * P
+                nc.sync.dma_start(out[:, at : at + 2 * P], last_two[:, rank, :])
 
         gather_words(0)
         for t in range(TILES):

@@ -24,7 +24,6 @@ MULT = mybir.AluOpType.mult
 
 ROW = 2 * H
 SHIFT = 16
-LIVE_SPAN = 100
 
 
 def tile_moe_pke_glu_silu_kernel(
@@ -96,10 +95,11 @@ def tile_moe_pke_glu_silu_kernel(
         load_experts(later, 1, 2, 1, 0)
         load_window(1)
         load_experts(later, 1, 3, 1, 0)
-        nc.sync.dma_start(xs_pass1[0:LIVE_SPAN, :].bitcast(I32), xs_slots[SHIFT : SHIFT + LIVE_SPAN, :].bitcast(I32))
+        for r in range(4):
+            nc.sync.dma_start(xs_pass1[r:P:32, :].bitcast(I32), xs_slots[SHIFT + r : P : 32, :].bitcast(I32))
         load_experts(later, 1, 0, 1, 1)
-        load_experts(later, 1, 1, 1, 1)
-        load_experts(later, 1, 2, 2, 1)
+        load_experts(later, 1, 1, 2, 1)
+        load_experts(later, 1, 3, 1, 1)
         for pair in range(2):
             load_plane(w3_planes[pair], w3_scales.bitcast(I32)[2 * pair : 2 * pair + 2])
             for s in range(PASSES):

@@ -36,12 +36,12 @@ def tile_moe_pke_glu_silu_kernel(
 
         offsets = keep.tile([P, SLOTS // 16], U16, name="offsets")
 
-        xs_window = keep.tile([P, T], U8, name="xs_window", align_bytes=64)
-        xs_slots = keep.tile([P, SLOTS], U8, name="xs_slots", align_bytes=64)
-        xs_pass1 = keep.tile([P, SLOTS], U8, name="xs_pass1", align_bytes=64)
-        w1_plane = keep.tile([P, E * PASSES * H], U8, name="w1_plane", align_bytes=64)
-        w3_planes = [keep.tile([P, 2 * PASSES * H], U8, name="w3_plane%d" % pair, align_bytes=64) for pair in range(2)]
-        w2_plane = keep.tile([P, E * N], U8, name="w2_plane", align_bytes=64)
+        xs_window = keep.tile([P, T], U8, name="xs_window", align_bytes=256)
+        xs_slots = keep.tile([P, SLOTS], U8, name="xs_slots", align_bytes=256)
+        xs_pass1 = keep.tile([P, SLOTS], U8, name="xs_pass1", align_bytes=256)
+        w1_plane = keep.tile([P, E * PASSES * H], U8, name="w1_plane", align_bytes=256)
+        w3_planes = [keep.tile([P, 2 * PASSES * H], U8, name="w3_plane%d" % pair, align_bytes=256) for pair in range(2)]
+        w2_plane = keep.tile([P, E * N], U8, name="w2_plane", align_bytes=256)
         ident = keep.tile([P, P], F32, name="ident")
 
         make_identity(nc, ident[:])
@@ -61,7 +61,7 @@ def tile_moe_pke_glu_silu_kernel(
                 nc.sync.dma_start(plane[r:P:32, :].bitcast(I32).rearrange("q (g i) -> q g i", g=rows.shape[2]), rows[r])
 
         def load_rows(pool, name, rows):
-            tile = pool.tile([P, rows.shape[0] * rows.shape[2] * 4], U8, name=name, align_bytes=64)
+            tile = pool.tile([P, rows.shape[0] * rows.shape[2] * 4], U8, name=name, align_bytes=256)
             nc.sync.dma_start(tile[:].bitcast(I32).rearrange("p (g b) -> p g b", g=rows.shape[0]), rows.rearrange("g p b -> p g b"))
             return tile
 
@@ -72,7 +72,7 @@ def tile_moe_pke_glu_silu_kernel(
         windows = {}
 
         def load_window(s):
-            windows[s] = later.tile([P, T], I32, name="x%d" % s, align_bytes=64)
+            windows[s] = later.tile([P, T], I32, name="x%d" % s, align_bytes=256)
             nc.sync.dma_start(windows[s][:], x_rows[s])
 
         def load_experts(pool, which, first, count, s):
@@ -113,7 +113,7 @@ def tile_moe_pke_glu_silu_kernel(
 
         def gather_words(s):
             for e in range(E):
-                gathered[(s, e)] = keep.tile([P, C], U32, name="xg%d_%d" % (s, e), align_bytes=64)
+                gathered[(s, e)] = keep.tile([P, C], U32, name="xg%d_%d" % (s, e), align_bytes=256)
                 picks = offsets[:, e * C // 16 : (e + 1) * C // 16]
                 nc.vector.tensor_copy(gathered[(s, e)][:], windows[s][:].bitcast(U32).indirect(picks))
 
@@ -162,13 +162,13 @@ def tile_moe_pke_glu_silu_kernel(
                 for u in range(2):
                     at = u * width + j * P
                     nc.tensor.transpose(turned[:, at : at + P], pairs[:, u * P : (u + 1) * P], ident[:])
-            rows = keep.tile([P, 4 * width], BF16, name="rows%d" % tiles[0], align_bytes=64)
+            rows = keep.tile([P, 4 * width], BF16, name="rows%d" % tiles[0], align_bytes=256)
             copy_out(
                 rows[:].bitcast(F32).rearrange("p (c u) -> p c u", u=2),
                 turned[:, : 2 * width].rearrange("p (u c) -> p c u", u=2),
             )
-            codes = keep.tile([P, width], U32, name="codes%d" % tiles[0], align_bytes=64)
-            scales = keep.tile([P, width], U8, name="scales%d" % tiles[0], align_bytes=64)
+            codes = keep.tile([P, width], U32, name="codes%d" % tiles[0], align_bytes=256)
+            scales = keep.tile([P, width], U8, name="scales%d" % tiles[0], align_bytes=256)
             nc.vector.quantize_mx(out=codes[:].bitcast(FP8X4), scales=scales[:], in_=rows[:])
             packed[tiles] = (codes, scales)
 

@@ -24,6 +24,7 @@ MULT = mybir.AluOpType.mult
 
 ROW = 2 * H
 SHIFT = 16
+ALIGN = 256
 
 
 def tile_moe_pke_glu_silu_kernel(
@@ -34,15 +35,20 @@ def tile_moe_pke_glu_silu_kernel(
         keep = ctx.enter_context(tc.tile_pool(name="keep", bufs=1))
         psum = ctx.enter_context(tc.psum_pool(name="psum", bufs=1))
 
-        offsets = keep.tile([P, SLOTS // 16], U16, name="offsets")
+        def sbuf(pool, shape, dtype, name):
+            return pool.tile(shape, dtype, name=name, align_bytes=ALIGN)
 
-        xs_window = keep.tile([P, T], U8, name="xs_window", align_bytes=256)
-        xs_slots = keep.tile([P, SLOTS], U8, name="xs_slots", align_bytes=256)
-        xs_pass1 = keep.tile([P, SLOTS], U8, name="xs_pass1", align_bytes=256)
-        w1_plane = keep.tile([P, E * PASSES * H], U8, name="w1_plane", align_bytes=256)
-        w3_planes = [keep.tile([P, 2 * PASSES * H], U8, name="w3_plane%d" % pair, align_bytes=256) for pair in range(2)]
-        w2_plane = keep.tile([P, E * N], U8, name="w2_plane", align_bytes=256)
-        ident = keep.tile([P, P], F32, name="ident")
+        offsets = sbuf(keep, [P, SLOTS // 16], U16, "offsets")
+        xs_window = sbuf(keep, [P, T], U8, "xs_window")
+        xs_slots = sbuf(keep, [P, SLOTS], U8, "xs_slots")
+        xs_pass1 = sbuf(keep, [P, SLOTS], U8, "xs_pass1")
+        planes = {
+            (which, pair): sbuf(keep, [P, 2 * PASSES * H], U8, "plane%d_%d" % (which, pair))
+            for pair in range(2)
+            for which in (1, 3)
+        }
+        w2_plane = sbuf(keep, [P, E * N], U8, "w2_plane")
+        ident = sbuf(keep, [P, P], F32, "ident")
 
         make_identity(nc, ident[:])
         with tc.tile_pool(name="zero", bufs=1) as scratch:
@@ -51,7 +57,7 @@ def tile_moe_pke_glu_silu_kernel(
             nc.vector.memset(xs_window[:].bitcast(I32), 0)
             cleared = xs_pass1[:].bitcast(I32)
             nc.vector.tensor_copy(cleared, zero[:].to_broadcast(cleared.shape))
-        for plane in [w1_plane] + w3_planes + [w2_plane]:
+        for plane in list(planes.values()) + [w2_plane]:
             nc.vector.memset(plane[:].bitcast(I32), 0)
         later = ctx.enter_context(tc.tile_pool(name="later", bufs=1))
 
@@ -61,18 +67,19 @@ def tile_moe_pke_glu_silu_kernel(
                 nc.sync.dma_start(plane[r:P:32, :].bitcast(I32).rearrange("q (g i) -> q g i", g=rows.shape[2]), rows[r])
 
         def load_rows(pool, name, rows):
-            tile = pool.tile([P, rows.shape[0] * rows.shape[2] * 4], U8, name=name, align_bytes=256)
+            tile = sbuf(pool, [P, rows.shape[0] * rows.shape[2] * 4], U8, name)
             nc.sync.dma_start(tile[:].bitcast(I32).rearrange("p (g b) -> p g b", g=rows.shape[0]), rows.rearrange("g p b -> p g b"))
             return tile
 
         x_rows = x_words.rearrange("s p t r -> s p (t r)").bitcast(I32)
         xs_rows = x_scales.bitcast(I32).rearrange("s (q r) t -> r q s t", r=4)
         word_rows = {1: w1_words.bitcast(I32), 3: w3_words.bitcast(I32)}
+        scale_rows = {1: w1_scales.bitcast(I32), 3: w3_scales.bitcast(I32)}
         weights = {}
         windows = {}
 
         def load_window(s):
-            windows[s] = later.tile([P, T], I32, name="x%d" % s, align_bytes=256)
+            windows[s] = sbuf(later, [P, T], I32, "x%d" % s)
             nc.sync.dma_start(windows[s][:], x_rows[s])
 
         def load_experts(pool, which, first, count, s):
@@ -85,26 +92,30 @@ def tile_moe_pke_glu_silu_kernel(
             for s in range(PASSES):
                 weights[(which, e, s)] = tile[:, s * ROW : (s + 1) * ROW]
 
+        def load_scales(which, pair):
+            load_plane(planes[(which, pair)], scale_rows[which][2 * pair : 2 * pair + 2])
+
         load_experts(keep, 1, 0, 2, 0)
         nc.sync.dma_start(offsets[:], offs)
         for r in range(4):
             nc.sync.dma_start(xs_window[r:P:SHIFT, :].bitcast(I32), xs_rows[r])
         nc.vector.tensor_copy(xs_slots[:], xs_window[:].indirect(offsets[:]))
         load_window(0)
-        load_plane(w1_plane, w1_scales.bitcast(I32))
-        load_experts(later, 1, 2, 1, 0)
+        load_scales(1, 0)
+        load_experts(later, 3, 0, 2, 0)
+        load_scales(3, 0)
         load_window(1)
-        load_experts(later, 1, 3, 1, 0)
         for r in range(4):
             nc.sync.dma_start(xs_pass1[r:P:32, :].bitcast(I32), xs_slots[SHIFT + r : P : 32, :].bitcast(I32))
-        load_experts(later, 1, 0, 1, 1)
-        load_experts(later, 1, 1, 2, 1)
-        load_experts(later, 1, 3, 1, 1)
-        for pair in range(2):
-            load_plane(w3_planes[pair], w3_scales.bitcast(I32)[2 * pair : 2 * pair + 2])
+        for e in range(2):
+            for which in (1, 3):
+                load_experts(later, which, e, 1, 1)
+        for which in (1, 3):
+            load_scales(which, 1)
             for s in range(PASSES):
-                load_experts(later, 3, 2 * pair, 1, s)
-            load_both_passes(3, 2 * pair + 1)
+                load_experts(later, which, 2, 1, s)
+        for which in (1, 3):
+            load_both_passes(which, 3)
         w2_all = load_rows(later, "w2_all", w2_words.bitcast(I32)[:, 0])
         load_plane(w2_plane, w2_scales.bitcast(I32))
 
@@ -113,7 +124,7 @@ def tile_moe_pke_glu_silu_kernel(
 
         def gather_words(s):
             for e in range(E):
-                gathered[(s, e)] = keep.tile([P, C], U32, name="xg%d_%d" % (s, e), align_bytes=256)
+                gathered[(s, e)] = sbuf(keep, [P, C], U32, "xg%d_%d" % (s, e))
                 picks = offsets[:, e * C // 16 : (e + 1) * C // 16]
                 nc.vector.tensor_copy(gathered[(s, e)][:], windows[s][:].bitcast(U32).indirect(picks))
 
@@ -122,20 +133,15 @@ def tile_moe_pke_glu_silu_kernel(
 
         sums = {}
 
-        def first_layer(t, which, s):
+        def first_layer(t, which, s, lo=0, hi=H):
             e, rank = divmod(t, RANKS)
-            if s == 0:
-                sums[(t, which)] = bank(t)
-            if which == 1:
-                plane, g = w1_plane, e * PASSES + s
-            else:
-                plane, g = w3_planes[e // 2], e % 2 * PASSES + s
+            g = e % 2 * PASSES + s
             nc.tensor.matmul_mx(
-                out=sums[(t, which)][:],
+                out=sums[(t, which, lo)][:, : hi - lo],
                 lhsT=gathered[(s, e)][:, rank * P : (rank + 1) * P].bitcast(FP8X4),
                 lhsT_scale=x_plane[s][:, t * P : (t + 1) * P],
-                rhs=weights[(which, e, s)].bitcast(FP4X4),
-                rhs_scale=plane[:, g * H : (g + 1) * H],
+                rhs=weights[(which, e, s)][:, 2 * lo : 2 * hi].bitcast(FP4X4),
+                rhs_scale=planes[(which, e // 2)][:, g * H + lo : g * H + hi],
                 start=(s == 0),
                 stop=(s == PASSES - 1),
             )
@@ -145,81 +151,105 @@ def tile_moe_pke_glu_silu_kernel(
         hidden = {}
 
         def silu(t):
-            gates[t] = keep.tile([P, 2, P, 2], F32, name="gate%d" % t)
-            nc.scalar.activation(gates[t][:], sums[(t, 1)][:].rearrange(order, u=2, d=2), SILU)
+            gates[t] = sbuf(keep, [P, 2, P, 2], F32, "gate%d" % t)
+            nc.scalar.activation(gates[t][:], sums[(t, 1, 0)][:].rearrange(order, u=2, d=2), SILU)
 
-        def gate(t):
-            hidden[t] = keep.tile([P, 2, P, 2], BF16, name="hidden%d" % t)
-            nc.vector.tensor_tensor(hidden[t][:], gates[t][:], sums[(t, 3)][:].rearrange(order, u=2, d=2), MULT)
+        def gate(t, lo=0, hi=H):
+            if lo == 0:
+                hidden[t] = sbuf(keep, [P, 2, P, 2], BF16, "hidden%d" % t)
+            part = slice(lo // 4, hi // 4)
+            nc.vector.tensor_tensor(
+                hidden[t][:, :, part, :],
+                gates[t][:, :, part, :],
+                sums[(t, 3, lo)][:, : hi - lo].rearrange(order, u=2, d=2),
+                MULT,
+            )
 
-        packed = {}
+        rows = {e: sbuf(keep, [P, 4 * C], BF16, "rows%d" % e) for e in range(E)}
+        codes = {e: sbuf(keep, [P, C], U32, "codes%d" % e) for e in range(E)}
+        scales = {e: sbuf(keep, [P, C], U8, "scales%d" % e) for e in range(E)}
 
         def turn(tiles, bank_number, copy_out):
             width = len(tiles) * P
+            e, rank = divmod(tiles[0], RANKS)
             turned = bank(bank_number)
             for j, t in enumerate(tiles):
                 pairs = hidden[t][:].rearrange("c u p d -> c (u p d)").bitcast(F32)
                 for u in range(2):
                     at = u * width + j * P
                     nc.tensor.transpose(turned[:, at : at + P], pairs[:, u * P : (u + 1) * P], ident[:])
-            rows = keep.tile([P, 4 * width], BF16, name="rows%d" % tiles[0], align_bytes=256)
             copy_out(
-                rows[:].bitcast(F32).rearrange("p (c u) -> p c u", u=2),
+                rows[e][:, 4 * rank * P : 4 * (rank * P + width)].bitcast(F32).rearrange("p (c u) -> p c u", u=2),
                 turned[:, : 2 * width].rearrange("p (u c) -> p c u", u=2),
             )
-            codes = keep.tile([P, width], U32, name="codes%d" % tiles[0], align_bytes=256)
-            scales = keep.tile([P, width], U8, name="scales%d" % tiles[0], align_bytes=256)
-            nc.vector.quantize_mx(out=codes[:].bitcast(FP8X4), scales=scales[:], in_=rows[:])
-            packed[tiles] = (codes, scales)
+
+        def quantise(e, lo, hi):
+            nc.vector.quantize_mx(out=codes[e][:, lo:hi].bitcast(FP8X4), scales=scales[e][:, lo:hi], in_=rows[e][:, 4 * lo : 4 * hi])
 
         by_rank = out.rearrange("n (m e u) -> n e m u", m=RANKS, e=E)
-        last_two = keep.tile([P, RANKS, 2 * P], F32, name="last_two")
+        results = {e: sbuf(keep, [P, C], F32, "result%d" % e) for e in range(E)}
 
-        def second_layer(tiles, bank_number, copy_out):
-            width = len(tiles) * P
-            e = tiles[0] // RANKS
-            codes, scales = packed[tiles]
+        def second_layer(e, lo, hi, bank_number, copy_out):
             product = bank(bank_number)
             nc.tensor.matmul_mx(
-                out=product[:, :width],
+                out=product[:, : hi - lo],
                 lhsT=w2_all[:, e * 2 * N : (e + 1) * 2 * N].bitcast(FP4X4),
                 lhsT_scale=w2_plane[:, e * N : (e + 1) * N],
-                rhs=codes[:].bitcast(FP8X4),
-                rhs_scale=scales[:],
+                rhs=codes[e][:, lo:hi].bitcast(FP8X4),
+                rhs_scale=scales[e][:, lo:hi],
                 start=True,
                 stop=True,
             )
-            if e < 2:
-                result = keep.tile([P, RANKS, P], F32, name="result%d" % e)
-                copy_out(result[:], product[:, :C].rearrange("n (m u) -> n m u", u=P))
-                nc.sync.dma_start(by_rank[:, e], result[:])
-            elif e == 2:
-                copy_out(last_two[:, :, :P], product[:, :C].rearrange("n (m u) -> n m u", u=P))
-            else:
-                rank = tiles[0] % RANKS
-                copy_out(last_two[:, rank, P:], product[:, :P])
-                at = rank * E * P + 2 * P
-                nc.sync.dma_start(out[:, at : at + 2 * P], last_two[:, rank, :])
+            copy_out(results[e][:, lo:hi], product[:, : hi - lo])
+            if hi == C:
+                nc.sync.dma_start(by_rank[:, e], results[e][:].rearrange("n (m u) -> n m u", u=P))
 
         gather_words(0)
-        for t in range(TILES):
-            first_layer(t, 1, 0)
+        for which, first_bank in ((1, 0), (3, 4)):
+            for t in range(4):
+                sums[(t, which, 0)] = bank(first_bank + t)
+                first_layer(t, which, 0)
         gather_words(1)
-        for t in range(TILES):
-            first_layer(t, 1, 1)
+        for e in range(2):
+            for which, after in ((1, silu), (3, gate)):
+                for t in (2 * e, 2 * e + 1):
+                    first_layer(t, which, 1)
+                    after(t)
+        for which, first_bank, after in ((1, 0, silu), (3, 4, gate)):
+            for s in range(PASSES):
+                for t in (4, 5):
+                    if s == 0:
+                        sums[(t, which, 0)] = bank(first_bank + t - 4)
+                    first_layer(t, which, s)
+                    if s == PASSES - 1:
+                        after(t)
+        for t in (6, 7):
+            sums[(t, 1, 0)] = bank(t - 4)
+            for s in range(PASSES):
+                first_layer(t, 1, s)
             silu(t)
-        for e in range(E):
-            tiles = (RANKS * e, RANKS * e + 1)
-            if e % 2 == 0:
-                steps = [(t, s) for s in range(PASSES) for t in tiles]
-            else:
-                steps = [(t, s) for t in tiles for s in range(PASSES)]
-            for t, s in steps:
-                first_layer(t, 3, s)
-                if s == PASSES - 1:
-                    gate(t)
-        groups = [(0, 1), (2, 3), (4, 5), (6,), (7,)]
-        for tiles, bank_number in zip(groups, (4, 5, 0, 1, 2)):
-            turn(tiles, bank_number, nc.vector.tensor_copy if tiles == (2, 3) else nc.scalar.copy)
-        for tiles, bank_number in zip(groups, (3, 6, 7, 4, 5)):
-            second_layer(tiles, bank_number, nc.vector.tensor_copy if len(tiles) == 1 else nc.scalar.copy)
+        halves = [(t, lo) for t in (6, 7) for lo in (0, H // 2)]
+        for (t, lo), bank_number in zip(halves, (6, 7, 0, 1)):
+            sums[(t, 3, lo)] = bank(bank_number)
+            for s in range(PASSES):
+                first_layer(t, 3, s, lo, lo + H // 2)
+            gate(t, lo, lo + H // 2)
+
+        on_vector, on_scalar = nc.vector.tensor_copy, nc.scalar.copy
+        turn((0,), 2, on_vector)
+        turn((1,), 3, on_scalar)
+        quantise(0, 0, C)
+        turn((2, 3), 6, on_scalar)
+        turn((4,), 7, on_vector)
+        quantise(1, 0, C)
+        turn((5,), 0, on_scalar)
+        quantise(2, 0, C)
+        turn((6,), 4, on_scalar)
+        quantise(3, 0, P)
+        turn((7,), 5, on_scalar)
+        quantise(3, P, C)
+        second_layer(0, 0, C, 1, on_scalar)
+        second_layer(1, 0, C, 2, on_scalar)
+        second_layer(2, 0, C, 3, on_scalar)
+        second_layer(3, 0, P, 6, on_vector)
+        second_layer(3, P, C, 7, on_vector)

@@ -165,13 +165,20 @@ def tile_moe_pke_glu_silu_kernel(
                 MULT,
             )
 
-        rows = {e: sbuf(keep, [P, 4 * C], BF16, "rows%d" % e) for e in range(E)}
-        codes = {e: sbuf(keep, [P, C], U32, "codes%d" % e) for e in range(E)}
-        scales = {e: sbuf(keep, [P, C], U8, "scales%d" % e) for e in range(E)}
+        groups = [(0, 2), (1, 3), (4, 6), (5, 7)]
+        place = {t: (g, j) for g, tiles in enumerate(groups) for j, t in enumerate(tiles)}
+        rows = [sbuf(keep, [P, 8 * P], BF16, "rows%d" % g) for g in range(len(groups))]
+        codes = [sbuf(keep, [P, 2 * P], U32, "codes%d" % g) for g in range(len(groups))]
+        scales = [sbuf(keep, [P, 2 * P], U8, "scales%d" % g) for g in range(len(groups))]
+        results = [sbuf(keep, [P, 2 * P], F32, "result%d" % g) for g in range(len(groups))]
+
+        def span(tiles):
+            g, j = place[tiles[0]]
+            return g, j * P, (j + len(tiles)) * P
 
         def turn(tiles, bank_number, copy_out):
-            width = len(tiles) * P
-            e, rank = divmod(tiles[0], RANKS)
+            g, lo, hi = span(tiles)
+            width = hi - lo
             turned = bank(bank_number)
             for j, t in enumerate(tiles):
                 pairs = hidden[t][:].rearrange("c u p d -> c (u p d)").bitcast(F32)
@@ -179,30 +186,34 @@ def tile_moe_pke_glu_silu_kernel(
                     at = u * width + j * P
                     nc.tensor.transpose(turned[:, at : at + P], pairs[:, u * P : (u + 1) * P], ident[:])
             copy_out(
-                rows[e][:, 4 * rank * P : 4 * (rank * P + width)].bitcast(F32).rearrange("p (c u) -> p c u", u=2),
+                rows[g][:, 4 * lo : 4 * hi].bitcast(F32).rearrange("p (c u) -> p c u", u=2),
                 turned[:, : 2 * width].rearrange("p (u c) -> p c u", u=2),
             )
 
-        def quantise(e, lo, hi):
-            nc.vector.quantize_mx(out=codes[e][:, lo:hi].bitcast(FP8X4), scales=scales[e][:, lo:hi], in_=rows[e][:, 4 * lo : 4 * hi])
+        def quantise(tiles):
+            g, lo, hi = span(tiles)
+            nc.vector.quantize_mx(out=codes[g][:, lo:hi].bitcast(FP8X4), scales=scales[g][:, lo:hi], in_=rows[g][:, 4 * lo : 4 * hi])
 
-        by_rank = out.rearrange("n (m e u) -> n e m u", m=RANKS, e=E)
-        results = {e: sbuf(keep, [P, C], F32, "result%d" % e) for e in range(E)}
-
-        def second_layer(e, lo, hi, bank_number, copy_out):
+        def second_layer(tiles, bank_number, copy_out):
+            g, lo, hi = span(tiles)
             product = bank(bank_number)
-            nc.tensor.matmul_mx(
-                out=product[:, : hi - lo],
-                lhsT=w2_all[:, e * 2 * N : (e + 1) * 2 * N].bitcast(FP4X4),
-                lhsT_scale=w2_plane[:, e * N : (e + 1) * N],
-                rhs=codes[e][:, lo:hi].bitcast(FP8X4),
-                rhs_scale=scales[e][:, lo:hi],
-                start=True,
-                stop=True,
-            )
-            copy_out(results[e][:, lo:hi], product[:, : hi - lo])
-            if hi == C:
-                nc.sync.dma_start(by_rank[:, e], results[e][:].rearrange("n (m u) -> n m u", u=P))
+            for j, t in enumerate(tiles):
+                e = t // RANKS
+                columns = slice(lo + j * P, lo + (j + 1) * P)
+                nc.tensor.matmul_mx(
+                    out=product[:, j * P : (j + 1) * P],
+                    lhsT=w2_all[:, e * 2 * N : (e + 1) * 2 * N].bitcast(FP4X4),
+                    lhsT_scale=w2_plane[:, e * N : (e + 1) * N],
+                    rhs=codes[g][:, columns].bitcast(FP8X4),
+                    rhs_scale=scales[g][:, columns],
+                    start=True,
+                    stop=True,
+                )
+            copy_out(results[g][:, lo:hi], product[:, : hi - lo])
+            if hi == 2 * P:
+                e, rank = divmod(groups[g][0], RANKS)
+                at = (rank * E + e) * P
+                nc.sync.dma_start(out[:, at : at + 2 * P], results[g][:])
 
         gather_words(0)
         for which, first_bank in ((1, 0), (3, 4)):
@@ -237,19 +248,19 @@ def tile_moe_pke_glu_silu_kernel(
 
         on_vector, on_scalar = nc.vector.tensor_copy, nc.scalar.copy
         turn((0,), 2, on_vector)
-        turn((1,), 3, on_scalar)
-        quantise(0, 0, C)
-        turn((2, 3), 6, on_scalar)
+        turn((2,), 3, on_scalar)
+        quantise((0, 2))
+        turn((1, 3), 6, on_scalar)
         turn((4,), 7, on_vector)
-        quantise(1, 0, C)
-        turn((5,), 0, on_scalar)
-        quantise(2, 0, C)
+        quantise((1, 3))
         turn((6,), 4, on_scalar)
-        quantise(3, 0, P)
+        quantise((4, 6))
+        turn((5,), 0, on_scalar)
+        quantise((5,))
         turn((7,), 5, on_scalar)
-        quantise(3, P, C)
-        second_layer(0, 0, C, 1, on_scalar)
-        second_layer(1, 0, C, 2, on_scalar)
-        second_layer(2, 0, C, 3, on_scalar)
-        second_layer(3, 0, P, 6, on_vector)
-        second_layer(3, P, C, 7, on_vector)
+        quantise((7,))
+        second_layer((0, 2), 1, on_scalar)
+        second_layer((1, 3), 2, on_scalar)
+        second_layer((4, 6), 3, on_scalar)
+        second_layer((5,), 6, on_vector)
+        second_layer((7,), 7, on_vector)

@@ -23,7 +23,7 @@ SILU = mybir.ActivationFunctionType.Silu
 MULT = mybir.AluOpType.mult
 
 ROW = 2 * H
-SHIFT = 16
+PASS1_FIRST, PASS1_STEP = 4, 8
 ALIGN = 256
 
 
@@ -72,7 +72,7 @@ def tile_moe_pke_glu_silu_kernel(
             return tile
 
         x_rows = x_words.rearrange("s p t r -> s p (t r)").bitcast(I32)
-        xs_rows = x_scales.bitcast(I32).rearrange("s (q r) t -> r q s t", r=4)
+        xs_rows = x_scales.bitcast(I32)
         word_rows = {1: w1_words.bitcast(I32), 3: w3_words.bitcast(I32)}
         scale_rows = {1: w1_scales.bitcast(I32), 3: w3_scales.bitcast(I32)}
         weights = {}
@@ -95,10 +95,13 @@ def tile_moe_pke_glu_silu_kernel(
         def load_scales(which, pair):
             load_plane(planes[(which, pair)], scale_rows[which][2 * pair : 2 * pair + 2])
 
-        load_experts(keep, 1, 0, 2, 0)
+        first = load_rows(keep, "w1_first", word_rows[1].rearrange("e s p b -> (e s) p b")[:3])
+        for g in range(3):
+            weights[(1,) + divmod(g, PASSES)] = first[:, g * ROW : (g + 1) * ROW]
         nc.sync.dma_start(offsets[:], offs)
+        nc.sync.dma_start(xs_window[PASS1_FIRST:P:PASS1_STEP, :].bitcast(I32), xs_rows[1])
         for r in range(4):
-            nc.sync.dma_start(xs_window[r:P:SHIFT, :].bitcast(I32), xs_rows[r])
+            nc.sync.dma_start(xs_window[r:P:32, :].bitcast(I32), xs_rows[0, r::4])
         nc.vector.tensor_copy(xs_slots[:], xs_window[:].indirect(offsets[:]))
         load_window(0)
         load_scales(1, 0)
@@ -106,10 +109,9 @@ def tile_moe_pke_glu_silu_kernel(
         load_scales(3, 0)
         load_window(1)
         for r in range(4):
-            nc.sync.dma_start(xs_pass1[r:P:32, :].bitcast(I32), xs_slots[SHIFT + r : P : 32, :].bitcast(I32))
-        for e in range(2):
-            for which in (1, 3):
-                load_experts(later, which, e, 1, 1)
+            nc.sync.dma_start(xs_pass1[r:P:32, :].bitcast(I32), xs_slots[PASS1_FIRST + PASS1_STEP * r : P : 32, :].bitcast(I32))
+        load_experts(later, 3, 0, 2, 1)
+        load_experts(later, 1, 1, 1, 1)
         for which in (1, 3):
             load_scales(which, 1)
             for s in range(PASSES):
@@ -122,11 +124,13 @@ def tile_moe_pke_glu_silu_kernel(
         x_plane = [xs_slots, xs_pass1]
         gathered = {}
 
-        def gather_words(s):
-            for e in range(E):
-                gathered[(s, e)] = sbuf(keep, [P, C], U32, "xg%d_%d" % (s, e))
-                picks = offsets[:, e * C // 16 : (e + 1) * C // 16]
-                nc.vector.tensor_copy(gathered[(s, e)][:], windows[s][:].bitcast(U32).indirect(picks))
+        def gather_words(s, cuts):
+            for lo, hi in zip(cuts, cuts[1:]):
+                words = sbuf(keep, [P, (hi - lo) * P], U32, "xg%d_%d" % (s, lo))
+                picks = offsets[:, lo * P // 16 : hi * P // 16]
+                nc.vector.tensor_copy(words[:], windows[s][:].bitcast(U32).indirect(picks))
+                for t in range(lo, hi):
+                    gathered[(s, t)] = words[:, (t - lo) * P : (t - lo + 1) * P]
 
         def bank(number):
             return psum.tile([P, H], F32, name="bank%d" % number)
@@ -134,11 +138,11 @@ def tile_moe_pke_glu_silu_kernel(
         sums = {}
 
         def first_layer(t, which, s, lo=0, hi=H):
-            e, rank = divmod(t, RANKS)
+            e = t // RANKS
             g = e % 2 * PASSES + s
             nc.tensor.matmul_mx(
                 out=sums[(t, which, lo)][:, : hi - lo],
-                lhsT=gathered[(s, e)][:, rank * P : (rank + 1) * P].bitcast(FP8X4),
+                lhsT=gathered[(s, t)].bitcast(FP8X4),
                 lhsT_scale=x_plane[s][:, t * P : (t + 1) * P],
                 rhs=weights[(which, e, s)][:, 2 * lo : 2 * hi].bitcast(FP4X4),
                 rhs_scale=planes[(which, e // 2)][:, g * H + lo : g * H + hi],
@@ -215,12 +219,12 @@ def tile_moe_pke_glu_silu_kernel(
                 at = (rank * E + e) * P
                 nc.sync.dma_start(out[:, at : at + 2 * P], results[g][:])
 
-        gather_words(0)
+        gather_words(0, (0, 2, 4, 6, 8))
         for which, first_bank in ((1, 0), (3, 4)):
             for t in range(4):
                 sums[(t, which, 0)] = bank(first_bank + t)
                 first_layer(t, which, 0)
-        gather_words(1)
+        gather_words(1, (0, 1, 2, 4, 6, 8))
         for e in range(2):
             for which, after in ((1, silu), (3, gate)):
                 for t in (2 * e, 2 * e + 1):

@@ -113,9 +113,9 @@ def tile_moe_pke_glu_silu_kernel(
         load_experts(later, 3, 0, 2, 1)
         load_experts(later, 1, 1, 1, 1)
         for which in (1, 3):
+            load_experts(later, which, 2, 1, 0)
             load_scales(which, 1)
-            for s in range(PASSES):
-                load_experts(later, which, 2, 1, s)
+            load_experts(later, which, 2, 1, 1)
         for which in (1, 3):
             load_both_passes(which, 3)
         w2_all = load_rows(later, "w2_all", w2_words.bitcast(I32)[:, 0])
@@ -124,8 +124,8 @@ def tile_moe_pke_glu_silu_kernel(
         x_plane = [xs_slots, xs_pass1]
         gathered = {}
 
-        def gather_words(s, cuts):
-            for lo, hi in zip(cuts, cuts[1:]):
+        def gather_words(s, spans):
+            for lo, hi in spans:
                 words = sbuf(keep, [P, (hi - lo) * P], U32, "xg%d_%d" % (s, lo))
                 picks = offsets[:, lo * P // 16 : hi * P // 16]
                 nc.vector.tensor_copy(words[:], windows[s][:].bitcast(U32).indirect(picks))
@@ -219,18 +219,18 @@ def tile_moe_pke_glu_silu_kernel(
                 at = (rank * E + e) * P
                 nc.sync.dma_start(out[:, at : at + 2 * P], results[g][:])
 
-        gather_words(0, (0, 2, 4, 6, 8))
+        gather_words(0, ((0, 2), (4, 6), (2, 4), (6, 8)))
         for which, first_bank in ((1, 0), (3, 4)):
             for t in range(4):
                 sums[(t, which, 0)] = bank(first_bank + t)
                 first_layer(t, which, 0)
-        gather_words(1, (0, 1, 2, 4, 6, 8))
+        gather_words(1, ((0, 1), (1, 2), (2, 4), (4, 6), (6, 8)))
         for e in range(2):
             for which, after in ((1, silu), (3, gate)):
                 for t in (2 * e, 2 * e + 1):
                     first_layer(t, which, 1)
                     after(t)
-        for which, first_bank, after in ((1, 0, silu), (3, 4, gate)):
+        for which, first_bank, after in ((1, 0, silu), (3, 2, gate)):
             for s in range(PASSES):
                 for t in (4, 5):
                     if s == 0:
@@ -239,7 +239,7 @@ def tile_moe_pke_glu_silu_kernel(
                     if s == PASSES - 1:
                         after(t)
         for t in (6, 7):
-            sums[(t, 1, 0)] = bank(t - 4)
+            sums[(t, 1, 0)] = bank(t - 2)
             for s in range(PASSES):
                 first_layer(t, 1, s)
             silu(t)
@@ -251,20 +251,20 @@ def tile_moe_pke_glu_silu_kernel(
             gate(t, lo, lo + H // 2)
 
         on_vector, on_scalar = nc.vector.tensor_copy, nc.scalar.copy
-        turn((0,), 2, on_vector)
-        turn((2,), 3, on_scalar)
+        turn((0,), 4, on_vector)
+        turn((2,), 5, on_scalar)
         quantise((0, 2))
         turn((1, 3), 6, on_scalar)
         turn((4,), 7, on_vector)
         quantise((1, 3))
-        turn((6,), 4, on_scalar)
+        turn((6,), 2, on_scalar)
         quantise((4, 6))
         turn((5,), 0, on_scalar)
         quantise((5,))
-        turn((7,), 5, on_scalar)
+        turn((7,), 3, on_scalar)
         quantise((7,))
         second_layer((0, 2), 1, on_scalar)
-        second_layer((1, 3), 2, on_scalar)
-        second_layer((4, 6), 3, on_scalar)
+        second_layer((1, 3), 4, on_scalar)
+        second_layer((4, 6), 5, on_scalar)
         second_layer((5,), 6, on_vector)
         second_layer((7,), 7, on_vector)

@@ -25,6 +25,7 @@ MULT = mybir.AluOpType.mult
 ROW = 2 * H
 PASS1_FIRST, PASS1_STEP = 4, 8
 ALIGN = 256
+SKEW = 32
 
 
 def tile_moe_pke_glu_silu_kernel(
@@ -126,9 +127,9 @@ def tile_moe_pke_glu_silu_kernel(
 
         def gather_words(s, spans):
             for lo, hi in spans:
-                words = sbuf(keep, [P, (hi - lo) * P], U32, "xg%d_%d" % (s, lo))
+                words = sbuf(keep, [P, SKEW + (hi - lo) * P], U32, "xg%d_%d" % (s, lo))[:, SKEW:]
                 picks = offsets[:, lo * P // 16 : hi * P // 16]
-                nc.vector.tensor_copy(words[:], windows[s][:].bitcast(U32).indirect(picks))
+                nc.vector.tensor_copy(words, windows[s][:].bitcast(U32).indirect(picks))
                 for t in range(lo, hi):
                     gathered[(s, t)] = words[:, (t - lo) * P : (t - lo + 1) * P]
 

from contextlib import ExitStack

import concourse.mybir as mybir
from concourse.masks import make_identity

K, T, E, C, H, N = 1024, 2048, 4, 256, 512, 128
RANKS = 2
SLOTS = E * C
P = 128
PASSES = K // 512
TILES = SLOTS // P
FLOPS = 2 * SLOTS * (2 * K * H + H * N)

F32 = mybir.dt.float32
BF16 = mybir.dt.bfloat16
I32 = mybir.dt.int32
U32 = mybir.dt.uint32
U16 = mybir.dt.uint16
U8 = mybir.dt.uint8
FP8X4 = mybir.dt.float8_e4m3fn_x4
FP4X4 = mybir.dt.float4_e2m1fn_x4
SILU = mybir.ActivationFunctionType.Silu
MULT = mybir.AluOpType.mult

ROW = 2 * H
PASS1_FIRST, PASS1_STEP = 4, 8
ALIGN = 256
SKEW = 32


def tile_moe_pke_glu_silu_kernel(
    tc, x_words, x_scales, w1_words, w1_scales, w3_words, w3_scales, w2_words, w2_scales, offs, out
):
    nc = tc.nc
    with ExitStack() as ctx:
        keep = ctx.enter_context(tc.tile_pool(name="keep", bufs=1))
        psum = ctx.enter_context(tc.psum_pool(name="psum", bufs=1))

        def sbuf(pool, shape, dtype, name):
            return pool.tile(shape, dtype, name=name, align_bytes=ALIGN)

        offsets = sbuf(keep, [P, SLOTS // 16], U16, "offsets")
        xs_window = sbuf(keep, [P, T], U8, "xs_window")
        xs_slots = sbuf(keep, [P, SLOTS], U8, "xs_slots")
        xs_pass1 = sbuf(keep, [P, SLOTS], U8, "xs_pass1")
        planes = {
            (which, pair): sbuf(keep, [P, 2 * PASSES * H], U8, "plane%d_%d" % (which, pair))
            for pair in range(2)
            for which in (1, 3)
        }
        w2_plane = sbuf(keep, [P, E * N], U8, "w2_plane")
        ident = sbuf(keep, [P, P], F32, "ident")

        make_identity(nc, ident[:])
        with tc.tile_pool(name="zero", bufs=1) as scratch:
            zero = scratch.tile([P, 1], I32, name="zero")
            nc.vector.memset(zero[:], 0)
            nc.vector.memset(xs_window[:].bitcast(I32), 0)
            cleared = xs_pass1[:].bitcast(I32)
            nc.vector.tensor_copy(cleared, zero[:].to_broadcast(cleared.shape))
        for plane in list(planes.values()) + [w2_plane]:
            nc.vector.memset(plane[:].bitcast(I32), 0)
        later = ctx.enter_context(tc.tile_pool(name="later", bufs=1))

        def load_plane(plane, scales):
            rows = scales.rearrange("e s (q r) i -> r q (e s) i", r=4)
            for r in range(4):
                nc.sync.dma_start(plane[r:P:32, :].bitcast(I32).rearrange("q (g i) -> q g i", g=rows.shape[2]), rows[r])

        def load_rows(pool, name, rows):
            tile = sbuf(pool, [P, rows.shape[0] * rows.shape[2] * 4], U8, name)
            nc.sync.dma_start(tile[:].bitcast(I32).rearrange("p (g b) -> p g b", g=rows.shape[0]), rows.rearrange("g p b -> p g b"))
            return tile

        x_rows = x_words.rearrange("s p t r -> s p (t r)").bitcast(I32)
        xs_rows = x_scales.bitcast(I32)
        word_rows = {1: w1_words.bitcast(I32), 3: w3_words.bitcast(I32)}
        scale_rows = {1: w1_scales.bitcast(I32), 3: w3_scales.bitcast(I32)}
        weights = {}
        windows = {}

        def load_window(s):
            windows[s] = sbuf(later, [P, T], I32, "x%d" % s)
            nc.sync.dma_start(windows[s][:], x_rows[s])

        def load_experts(pool, which, first, count, s):
            tile = load_rows(pool, "w%d_%d_%d" % (which, first, s), word_rows[which][first : first + count, s])
            for j in range(count):
                weights[(which, first + j, s)] = tile[:, j * ROW : (j + 1) * ROW]

        def load_both_passes(which, e):
            tile = load_rows(later, "w%d_%d" % (which, e), word_rows[which][e])
            for s in range(PASSES):
                weights[(which, e, s)] = tile[:, s * ROW : (s + 1) * ROW]

        def load_scales(which, pair):
            load_plane(planes[(which, pair)], scale_rows[which][2 * pair : 2 * pair + 2])

        first = load_rows(keep, "w1_first", word_rows[1].rearrange("e s p b -> (e s) p b")[:3])
        for g in range(3):
            weights[(1,) + divmod(g, PASSES)] = first[:, g * ROW : (g + 1) * ROW]
        nc.sync.dma_start(offsets[:], offs)
        nc.sync.dma_start(xs_window[PASS1_FIRST:P:PASS1_STEP, :].bitcast(I32), xs_rows[1])
        for r in range(4):
            nc.sync.dma_start(xs_window[r:P:32, :].bitcast(I32), xs_rows[0, r::4])
        nc.vector.tensor_copy(xs_slots[:], xs_window[:].indirect(offsets[:]))
        load_window(0)
        load_scales(1, 0)
        load_experts(later, 3, 0, 2, 0)
        load_scales(3, 0)
        load_window(1)
        for r in range(4):
            nc.sync.dma_start(xs_pass1[r:P:32, :].bitcast(I32), xs_slots[PASS1_FIRST + PASS1_STEP * r : P : 32, :].bitcast(I32))
        load_experts(later, 3, 0, 2, 1)
        load_experts(later, 1, 1, 1, 1)
        for which in (1, 3):
            load_experts(later, which, 2, 1, 0)
            load_scales(which, 1)
            load_experts(later, which, 2, 1, 1)
        for which in (1, 3):
            load_both_passes(which, 3)
        w2_all = load_rows(later, "w2_all", w2_words.bitcast(I32)[:, 0])
        load_plane(w2_plane, w2_scales.bitcast(I32))

        x_plane = [xs_slots, xs_pass1]
        gathered = {}

        def gather_words(s, spans):
            for lo, hi in spans:
                words = sbuf(keep, [P, SKEW + (hi - lo) * P], U32, "xg%d_%d" % (s, lo))[:, SKEW:]
                picks = offsets[:, lo * P // 16 : hi * P // 16]
                nc.vector.tensor_copy(words, windows[s][:].bitcast(U32).indirect(picks))
                for t in range(lo, hi):
                    gathered[(s, t)] = words[:, (t - lo) * P : (t - lo + 1) * P]

        def bank(number):
            return psum.tile([P, H], F32, name="bank%d" % number)

        sums = {}

        def first_layer(t, which, s, lo=0, hi=H):
            e = t // RANKS
            g = e % 2 * PASSES + s
            nc.tensor.matmul_mx(
                out=sums[(t, which, lo)][:, : hi - lo],
                lhsT=gathered[(s, t)].bitcast(FP8X4),
                lhsT_scale=x_plane[s][:, t * P : (t + 1) * P],
                rhs=weights[(which, e, s)][:, 2 * lo : 2 * hi].bitcast(FP4X4),
                rhs_scale=planes[(which, e // 2)][:, g * H + lo : g * H + hi],
                start=(s == 0),
                stop=(s == PASSES - 1),
            )

        order = "c (p u d) -> c u p d"
        gates = {}
        hidden = {}

        def silu(t):
            gates[t] = sbuf(keep, [P, 2, P, 2], F32, "gate%d" % t)
            nc.scalar.activation(gates[t][:], sums[(t, 1, 0)][:].rearrange(order, u=2, d=2), SILU)

        def gate(t, lo=0, hi=H):
            if lo == 0:
                hidden[t] = sbuf(keep, [P, 2, P, 2], BF16, "hidden%d" % t)
            part = slice(lo // 4, hi // 4)
            nc.vector.tensor_tensor(
                hidden[t][:, :, part, :],
                gates[t][:, :, part, :],
                sums[(t, 3, lo)][:, : hi - lo].rearrange(order, u=2, d=2),
                MULT,
            )

        groups = [(0, 2), (1, 3), (4, 6), (5, 7)]
        place = {t: (g, j) for g, tiles in enumerate(groups) for j, t in enumerate(tiles)}
        rows = [sbuf(keep, [P, 8 * P], BF16, "rows%d" % g) for g in range(len(groups))]
        codes = [sbuf(keep, [P, 2 * P], U32, "codes%d" % g) for g in range(len(groups))]
        scales = [sbuf(keep, [P, 2 * P], U8, "scales%d" % g) for g in range(len(groups))]
        results = [sbuf(keep, [P, 2 * P], F32, "result%d" % g) for g in range(len(groups))]

        def span(tiles):
            g, j = place[tiles[0]]
            return g, j * P, (j + len(tiles)) * P

        def turn(tiles, bank_number, copy_out):
            g, lo, hi = span(tiles)
            width = hi - lo
            turned = bank(bank_number)
            for j, t in enumerate(tiles):
                pairs = hidden[t][:].rearrange("c u p d -> c (u p d)").bitcast(F32)
                for u in range(2):
                    at = u * width + j * P
                    nc.tensor.transpose(turned[:, at : at + P], pairs[:, u * P : (u + 1) * P], ident[:])
            copy_out(
                rows[g][:, 4 * lo : 4 * hi].bitcast(F32).rearrange("p (c u) -> p c u", u=2),
                turned[:, : 2 * width].rearrange("p (u c) -> p c u", u=2),
            )

        def quantise(tiles):
            g, lo, hi = span(tiles)
            nc.vector.quantize_mx(out=codes[g][:, lo:hi].bitcast(FP8X4), scales=scales[g][:, lo:hi], in_=rows[g][:, 4 * lo : 4 * hi])

        def second_layer(tiles, bank_number, copy_out):
            g, lo, hi = span(tiles)
            product = bank(bank_number)
            for j, t in enumerate(tiles):
                e = t // RANKS
                columns = slice(lo + j * P, lo + (j + 1) * P)
                nc.tensor.matmul_mx(
                    out=product[:, j * P : (j + 1) * P],
                    lhsT=w2_all[:, e * 2 * N : (e + 1) * 2 * N].bitcast(FP4X4),
                    lhsT_scale=w2_plane[:, e * N : (e + 1) * N],
                    rhs=codes[g][:, columns].bitcast(FP8X4),
                    rhs_scale=scales[g][:, columns],
                    start=True,
                    stop=True,
                )
            copy_out(results[g][:, lo:hi], product[:, : hi - lo])
            if hi == 2 * P:
                e, rank = divmod(groups[g][0], RANKS)
                at = (rank * E + e) * P
                nc.sync.dma_start(out[:, at : at + 2 * P], results[g][:])

        gather_words(0, ((0, 2), (4, 6), (2, 4), (6, 8)))
        for which, first_bank in ((1, 0), (3, 4)):
            for t in range(4):
                sums[(t, which, 0)] = bank(first_bank + t)
                first_layer(t, which, 0)
        gather_words(1, ((0, 1), (1, 2), (2, 4), (4, 6), (6, 8)))
        for e in range(2):
            for which, after in ((1, silu), (3, gate)):
                for t in (2 * e, 2 * e + 1):
                    first_layer(t, which, 1)
                    after(t)
        for which, first_bank, after in ((1, 0, silu), (3, 2, gate)):
            for s in range(PASSES):
                for t in (4, 5):
                    if s == 0:
                        sums[(t, which, 0)] = bank(first_bank + t - 4)
                    first_layer(t, which, s)
                    if s == PASSES - 1:
                        after(t)
        for t in (6, 7):
            sums[(t, 1, 0)] = bank(t - 2)
            for s in range(PASSES):
                first_layer(t, 1, s)
            silu(t)
        halves = [(t, lo) for t in (6, 7) for lo in (0, H // 2)]
        for (t, lo), bank_number in zip(halves, (6, 7, 0, 1)):
            sums[(t, 3, lo)] = bank(bank_number)
            for s in range(PASSES):
                first_layer(t, 3, s, lo, lo + H // 2)
            gate(t, lo, lo + H // 2)

        on_vector, on_scalar = nc.vector.tensor_copy, nc.scalar.copy
        turn((0,), 4, on_vector)
        turn((2,), 5, on_scalar)
        quantise((0, 2))
        turn((1, 3), 6, on_scalar)
        turn((4,), 7, on_vector)
        quantise((1, 3))
        turn((6,), 2, on_scalar)
        quantise((4, 6))
        turn((5,), 0, on_scalar)
        quantise((5,))
        turn((7,), 3, on_scalar)
        quantise((7,))
        second_layer((0, 2), 1, on_scalar)
        second_layer((1, 3), 4, on_scalar)
        second_layer((4, 6), 5, on_scalar)
        second_layer((5,), 6, on_vector)
        second_layer((7,), 7, on_vector)
